import numpy as np
import ml_dtypes


def mxq(x, axis, fmt="e4m3"):
    dtype, down = {"e4m3": (ml_dtypes.float8_e4m3fn, 7), "e5m2": (ml_dtypes.float8_e5m2, 14)}[fmt]
    v = np.moveaxis(np.asarray(x, np.float32).astype(ml_dtypes.bfloat16).astype(np.float64), axis, -1)
    blocks = v.reshape(v.shape[:-1] + (-1, 32))
    amax = np.abs(blocks).max(-1, keepdims=True)
    byte = np.maximum(np.where(amax > 0, np.frexp(amax)[1] - 1 + 127, 0) - down, 1)
    scale = np.exp2(byte - 127.0)
    codes = (blocks / scale).astype(np.float32).astype(dtype).astype(np.float64)
    return np.moveaxis((codes * scale).reshape(v.shape), -1, axis)


WIDE = False


def mx_kscale(k):
    if not WIDE:
        return np.ones(k)
    levels = np.array([18, -18])
    if k % 512:
        return np.exp2(np.random.permutation(np.resize(levels, k // 32))).repeat(32)
    a = np.empty((k // 512, 16))
    for p in range(k // 512):
        a[p, :8] = np.random.permutation(np.resize(levels, 8))
        for g in range(8):
            far = levels[np.abs(levels - a[p, g]) >= 10]
            a[p, g + 8] = far[np.random.randint(len(far))]
    return np.exp2(a.ravel()).repeat(32)


def f64(x):
    return np.asarray(x).astype(np.float64)


def striped(idx):
    return np.tile(np.asarray(idx).reshape(-1, 16).T, (8, 1)).astype(np.uint16)


def unstriped(offs):
    return offs[:16].T.reshape(-1).astype(np.int64)


E2M1 = np.array([0.0, 0.5, 1.0, 1.5, 2.0, 3.0, 4.0, 6.0, -0.0, -0.5, -1.0, -1.5, -2.0, -3.0, -4.0, -6.0])


def pack_weight(w, fmt):
    k, n = w.shape
    w = f64(np.asarray(w, np.float32).astype(ml_dtypes.bfloat16)).reshape(k // 32, 32, n)
    amax = np.abs(w).max(1)
    if fmt == "e4m3":
        byte = np.frexp(amax)[1] - 1 + 127 - 7
    else:
        mant, ex = np.frexp(amax / 6.0)
        byte = np.where(mant > 0.5, ex, ex - 1) + 127
    byte = np.clip(np.where(amax > 0, byte, 1), 1, 254)
    scaled = (w * np.exp2(127.0 - byte)[:, None, :]).reshape(k, n).astype(np.float32)
    by_word = np.ascontiguousarray(scaled.reshape(k // 512, 128, 4, n).transpose(0, 1, 3, 2))
    if fmt == "e4m3":
        words = by_word.astype(ml_dtypes.float8_e4m3fn).view(np.uint8)
    else:
        c = by_word.astype(ml_dtypes.float4_e2m1fn).view(np.uint8) & 0xF
        words = (c[..., 0::2] | (c[..., 1::2] << 4)).reshape(k // 512, 128, 2 * n)
    return np.ascontiguousarray(words), np.ascontiguousarray(byte.astype(np.uint8).reshape(k // 512, 16, n))


def unpack_weight(words, scales, fmt):
    g, _, n = scales.shape
    words = np.ascontiguousarray(words).reshape(g, 128, n, -1)
    if fmt == "e4m3":
        vals = words.view(ml_dtypes.float8_e4m3fn).astype(np.float64)
    else:
        nib = np.empty((g, 128, n, 4), np.uint8)
        nib[..., 0::2] = words & 0xF
        nib[..., 1::2] = words >> 4
        vals = E2M1[nib]
    vals = vals * np.repeat(np.exp2(scales.astype(np.float64) - 127.0), 8, axis=1)[..., None]
    return vals.transpose(0, 1, 3, 2).reshape(g * 512, n)


B, N, T, D, R = 2, 512, 2048, 512, 512


def setup_inputs():
    n = np.random.standard_normal
    idx = np.random.permutation(T)[:B * N]
    s = mx_kscale(D)[:, None]
    z = mx_kscale(R)[:, None]
    r = np.random.uniform(0.5, 2.0, T)
    x = n((B, D, R))
    wp = pack_weight(n((D, T)) * (1.00 / np.sqrt(D)) / s / r, "e4m3")
    return {
        "xT": (x * s).astype(np.float32),
        "w_words": wp[0],
        "w_scales": wp[1],
        "y": np.random.randint(0, 2, (B, R, N)).astype(np.float32),
        "wt": (np.random.uniform(0.5, 1.5, (B, R, 1)) * 1.0 / np.sqrt(R) * z).astype(np.float32),
        "ts": np.tile(r, (128, 1)).astype(np.float32),
        "xm": (x.transpose(0, 2, 1) / z).astype(np.float32),
        "offs": striped(idx),
    }


def reference(xT, w_words, w_scales, y, wt, ts, xm, offs):
    idx = unstriped(offs)
    w = unpack_weight(w_words, w_scales, "e4m3")
    pick = lambda x: x[:, idx].reshape(x.shape[0], B, N).transpose(1, 0, 2)
    a = mxq(f64(xT), 1, "e4m3").transpose(0, 2, 1) @ pick(w)
    ts_ = pick(f64(ts))[:, :1, :]
    a = a * ts_
    g = f64(wt) * (1.0 / (1.0 + np.exp(-a)) - f64(y))
    g = g * ts_
    dw = mxq(f64(xm), 1, "e4m3").transpose(0, 2, 1) @ mxq(g, 1, "e5m2")
    gw = np.zeros((D, T))
    gw[:, idx] = dw.transpose(1, 0, 2).reshape(D, B * N)
    return gw

@@ -1,0 +1,222 @@
+from contextlib import ExitStack
+
+import concourse.mybir as mybir
+from concourse.masks import make_identity
+
+B, N, T, D, R = 2, 512, 2048, 512, 512
+FLOPS = 2 * 2 * B * N * D * R
+
+F32 = mybir.dt.float32
+BF16 = mybir.dt.bfloat16
+I32 = mybir.dt.int32
+U32 = mybir.dt.uint32
+U16 = mybir.dt.uint16
+U8 = mybir.dt.uint8
+E4M3 = mybir.dt.float8_e4m3fn_x4
+E5M2 = mybir.dt.float8_e5m2_x4
+ALU = mybir.AluOpType
+ACT = mybir.ActivationFunctionType
+
+P = 128
+PACK = 4
+LIST_COLS = N // 16
+NB = N // P
+DB = D // P
+
+
+def tile_attend_gnce_w_ts_kernel(tc, xT, w_words, w_scales, y, wt, ts, xm, offs, out):
+    nc = tc.nc
+    with ExitStack() as ctx:
+        keep = ctx.enter_context(tc.tile_pool(name="keep", bufs=1))
+        work = ctx.enter_context(tc.tile_pool(name="work", bufs=4))
+        psum = ctx.enter_context(tc.psum_pool(name="psum", bufs=2))
+
+        offsets = keep.tile([P, B * LIST_COLS], U16, name="offsets")
+        nc.sync.dma_start(offsets[:], offs)
+
+        def listed(b):
+            return offsets[:, b * LIST_COLS : (b + 1) * LIST_COLS]
+
+        word_table = keep.tile([P, T], I32, name="word_table", align_bytes=64)
+        nc.sync.dma_start(out=word_table[:], in_=w_words[0].rearrange("p t j -> p (t j)").bitcast(I32))
+
+        scale_table = keep.tile([P, T], U8, name="scale_table", align_bytes=64)
+        nc.vector.memset(scale_table[:].bitcast(I32), 0)
+        ts_table = keep.tile([P, T], F32, name="ts_table", align_bytes=64)
+        nc.vector.memset(ts_table[:], 0.0)
+        for q in range(4):
+            nc.scalar.dma_start(
+                out=scale_table[32 * q : 32 * q + 4, :].bitcast(I32),
+                in_=w_scales[0, 4 * q : 4 * q + 4, :].bitcast(I32),
+            )
+        nc.scalar.dma_start(out=ts_table[0:1, :], in_=ts[0:1, :])
+        wt_rows = keep.tile([P, B, PACK], F32, name="wt_rows")
+        nc.scalar.dma_start(out=wt_rows[:], in_=wt.rearrange("b (p j) o -> p b (j o)", j=PACK))
+
+        x_raw, y_raw, xm_raw = [], [], []
+        for b in range(B):
+            x_raw.append(keep.tile([P, PACK, R], F32, name="x_raw%d" % b))
+            y_raw.append(keep.tile([P, PACK, N], F32, name="y_raw%d" % b))
+            xm_raw.append(keep.tile([P, PACK, D], F32, name="xm_raw%d" % b))
+            nc.sync.dma_start(out=x_raw[b][:], in_=xT[b].rearrange("(p j) r -> p j r", j=PACK))
+            nc.sync.dma_start(out=y_raw[b][:], in_=y[b].rearrange("(c p) i -> p c i", p=P))
+            nc.sync.dma_start(out=xm_raw[b][:], in_=xm[b].rearrange("(p j) d -> p j d", j=PACK))
+
+        ident = keep.tile([P, P], F32, name="ident")
+        make_identity(nc, ident[:])
+        warm = keep.tile([P, 1], F32, name="warm")
+        nc.scalar.activation(out=warm[:], in_=ident[:, 0:1], func=ACT.Sigmoid)
+
+        windows = [keep.tile([P, T], F32, name="window%d" % k) for k in range(3)]
+
+        def interleave(engine_copy, grouped, raw, c0, c1):
+            engine_copy(
+                out=grouped[:, c0:c1, :].rearrange("p (c i) t -> p c t i", i=4),
+                in_=raw[:, :, c0:c1].rearrange("p t (c i) -> p c t i", i=4),
+            )
+
+        def mx_tiles(name, width):
+            codes = keep.tile([P, width], U32, name=name + "_codes", align_bytes=64)
+            scales = keep.tile([P, width], U8, name=name + "_scales", align_bytes=64)
+            return codes, scales
+
+        def quantize(pair, grouped, fmt, c0, c1):
+            nc.vector.quantize_mx(
+                out=pair[0][:, c0:c1].bitcast(fmt),
+                scales=pair[1][:, c0:c1],
+                in_=grouped[:, c0:c1, :].rearrange("p w t -> p (w t)"),
+            )
+
+        w_mx = [mx_tiles("w%d" % b, N) for b in range(B)]
+        x_mx = [mx_tiles("x%d" % b, R) for b in range(B)]
+        xm_mx = [mx_tiles("xm%d" % b, D) for b in range(B)]
+        h_mx = [mx_tiles("h%d" % b, N) for b in range(B)]
+        ts_listed = [keep.tile([P, N], F32, name="ts_listed%d" % b) for b in range(B)]
+        ts_col = [keep.tile([P, NB], F32, name="ts_col%d" % b) for b in range(B)]
+        wt_wide = [keep.tile([P, R], F32, name="wt_wide%d" % b) for b in range(B)]
+        x_grp = [keep.tile([P, R, PACK], BF16, name="x_grp%d" % b, align_bytes=64) for b in range(B)]
+        xm_grp = [keep.tile([P, D, PACK], BF16, name="xm_grp%d" % b, align_bytes=64) for b in range(B)]
+        h_grp = [keep.tile([P, N, PACK], BF16, name="h_grp%d" % b, align_bytes=64) for b in range(B)]
+        dw = [[keep.tile([P, N], F32, name="dw%d_%d" % (b, k)) for k in range(DB)] for b in range(B)]
+
+        def gather_scales(b):
+            nc.vector.tensor_copy(out=w_mx[b][1][:], in_=scale_table[:].indirect(listed(b)))
+
+        def gather_words(b):
+            nc.vector.tensor_copy(out=w_mx[b][0][:], in_=word_table[:].bitcast(U32).indirect(listed(b)))
+
+        def gather_ts(b):
+            nc.vector.tensor_copy(out=ts_listed[b][:], in_=ts_table[:].indirect(listed(b)))
+            bank = psum.tile([P, NB, P], F32, name="bank_out", tag="out")
+            for c in range(NB):
+                nc.tensor.transpose(bank[:, c, :], ts_listed[b][:, c * P : (c + 1) * P], ident[:])
+            nc.scalar.copy(out=ts_col[b][:], in_=bank[:, :, 0])
+
+        def spread_wt(b):
+            bank = psum.tile([P, PACK, P], F32, name="bank_wt", tag="out")
+            for j in range(PACK):
+                nc.tensor.transpose(bank[:, j, :], wt_rows[:, b, j : j + 1].to_broadcast([P, P]), ident[:])
+            nc.scalar.copy(out=wt_wide[b][:].rearrange("m (p j) -> m p j", j=PACK), in_=bank[:].rearrange("m j p -> m p j"))
+
+        def scores(b, c):
+            cols = slice(c * P, (c + 1) * P)
+            a = psum.tile([P, R], F32, name="bank_a", tag="a")
+            nc.tensor.matmul_mx(
+                out=a[:], lhsT=w_mx[b][0][:, cols].bitcast(E4M3), lhsT_scale=w_mx[b][1][:, cols],
+                rhs=x_mx[b][0][:].bitcast(E4M3), rhs_scale=x_mx[b][1][:], start=True, stop=True,
+            )
+            yt = psum.tile([P, PACK, P], F32, name="bank_y", tag="y")
+            for cr in range(PACK):
+                nc.tensor.transpose(yt[:, cr, :], y_raw[b][:, cr, cols], ident[:])
+            s = work.tile([P, R], F32, name="s")
+            nc.scalar.activation(out=s[:], in_=a[:], func=ACT.Sigmoid, scale=ts_col[b][:, c : c + 1])
+            diff = work.tile([P, R], F32, name="diff")
+            nc.vector.tensor_tensor(out=diff[:], in0=s[:], in1=yt[:].rearrange("m c p -> m (c p)"), op=ALU.subtract)
+            return diff
+
+        def weigh(b, c, diff):
+            h = work.tile([P, R], BF16, name="h", align_bytes=64)
+            nc.vector.scalar_tensor_tensor(
+                out=h[:], in0=diff[:], scalar=ts_col[b][:, c : c + 1], in1=wt_wide[b][:], op0=ALU.mult, op1=ALU.mult
+            )
+            return h
+
+        def turn(b, half, hs):
+            bank = psum.tile([P, 2, 2, P], F32, name="bank_h", tag="h")
+            for cc in range(2):
+                words = hs[cc][:].bitcast(F32)
+                for u in range(2):
+                    nc.tensor.transpose(bank[:, cc, u, :], words[:, u : 2 * P : 2], ident[:])
+            c0, c1 = half * 2 * P, (half + 1) * 2 * P
+            nc.scalar.copy(
+                out=h_grp[b][:, c0:c1, :].bitcast(F32).rearrange("p (c i) u -> p c i u", c=2),
+                in_=bank[:].rearrange("p c u i -> p c i u"),
+            )
+
+        def gradient(b):
+            diffs = [scores(b, 0), scores(b, 1)]
+            hs = [weigh(b, 0, diffs[0])]
+            diffs.append(scores(b, 2))
+            hs.append(weigh(b, 1, diffs[1]))
+            turn(b, 0, hs[0:2])
+            diffs.append(scores(b, 3))
+            hs.append(weigh(b, 2, diffs[2]))
+            quantize(h_mx[b], h_grp[b], E5M2, 0, 2 * P)
+            hs.append(weigh(b, 3, diffs[3]))
+            turn(b, 1, hs[2:4])
+
+        def product(b):
+            quantize(h_mx[b], h_grp[b], E5M2, 2 * P, 4 * P)
+            for k in range(DB):
+                cols = slice(k * P, (k + 1) * P)
+                acc = psum.tile([P, N], F32, name="bank_dw", tag="out")
+                nc.tensor.matmul_mx(
+                    out=acc[:], lhsT=xm_mx[b][0][:, cols].bitcast(E4M3), lhsT_scale=xm_mx[b][1][:, cols],
+                    rhs=h_mx[b][0][:].bitcast(E5M2), rhs_scale=h_mx[b][1][:], start=True, stop=True,
+                )
+                nc.scalar.copy(out=dw[b][k][:], in_=acc[:])
+
+        def scatter(b, k):
+            nc.vector.tensor_copy(out=windows[k % 3][:].indirect(listed(b)), in_=dw[b][k][:])
+
+        def store(k):
+            nc.sync.dma_start(out=out[k * P : (k + 1) * P, :], in_=windows[k % 3][:])
+
+        spread_wt(0)
+        gather_scales(0)
+        gather_ts(0)
+        gather_words(0)
+        interleave(nc.vector.tensor_copy, x_grp[0], x_raw[0], 0, 320)
+        interleave(nc.scalar.copy, x_grp[0], x_raw[0], 320, R)
+        quantize(x_mx[0], x_grp[0], E4M3, 0, R)
+        spread_wt(1)
+        interleave(nc.scalar.copy, xm_grp[0], xm_raw[0], 0, D // 2)
+        interleave(nc.scalar.copy, xm_grp[0], xm_raw[0], D // 2, D)
+        gradient(0)
+        quantize(xm_mx[0], xm_grp[0], E4M3, 0, D)
+        product(0)
+        gather_scales(1)
+        gather_ts(1)
+        gather_words(1)
+        interleave(nc.scalar.copy, x_grp[1], x_raw[1], 0, R // 2)
+        interleave(nc.scalar.copy, x_grp[1], x_raw[1], R // 2, R)
+        quantize(x_mx[1], x_grp[1], E4M3, 0, R)
+        interleave(nc.scalar.copy, xm_grp[1], xm_raw[1], 0, D // 2)
+        interleave(nc.scalar.copy, xm_grp[1], xm_raw[1], D // 2, D)
+        for window in windows:
+            nc.vector.memset(window[:], 0.0)
+        gradient(1)
+        quantize(xm_mx[1], xm_grp[1], E4M3, 0, D)
+        product(1)
+        scatter(0, 0)
+        scatter(1, 0)
+        store(0)
+        scatter(0, 1)
+        scatter(1, 1)
+        store(1)
+        scatter(0, 2)
+        scatter(1, 2)
+        store(2)
+        scatter(0, 3)
+        scatter(1, 3)
+        store(3)

@@ -28,8 +28,10 @@ def tile_attend_gnce_w_ts_kernel(tc, xT, w_words, w_scales, y, wt, ts, xm, offs,
     nc = tc.nc
     with ExitStack() as ctx:
         keep = ctx.enter_context(tc.tile_pool(name="keep", bufs=1))
-        work = ctx.enter_context(tc.tile_pool(name="work", bufs=4))
-        psum = ctx.enter_context(tc.psum_pool(name="psum", bufs=2))
+        psum = ctx.enter_context(tc.psum_pool(name="psum", bufs=1))
+
+        def sbuf(name, shape, dtype):
+            return keep.tile(shape, dtype, name=name, align_bytes=64)
 
         offsets = keep.tile([P, B * LIST_COLS], U16, name="offsets")
         nc.sync.dma_start(offsets[:], offs)
@@ -37,48 +39,78 @@ def tile_attend_gnce_w_ts_kernel(tc, xT, w_words, w_scales, y, wt, ts, xm, offs,
         def listed(b):
             return offsets[:, b * LIST_COLS : (b + 1) * LIST_COLS]
 
-        word_table = keep.tile([P, T], I32, name="word_table", align_bytes=64)
-        nc.sync.dma_start(out=word_table[:], in_=w_words[0].rearrange("p t j -> p (t j)").bitcast(I32))
-
-        scale_table = keep.tile([P, T], U8, name="scale_table", align_bytes=64)
-        nc.vector.memset(scale_table[:].bitcast(I32), 0)
-        ts_table = keep.tile([P, T], F32, name="ts_table", align_bytes=64)
+        scale_table = sbuf("scale_table", [P, T], U8)
+        nc.gpsimd.memset(scale_table[:].bitcast(I32), 0)
+        ts_table = keep.tile([P, T], F32, name="ts_table", tag="third", align_bytes=64)
         nc.vector.memset(ts_table[:], 0.0)
+        ident = sbuf("ident", [P, P], F32)
+        make_identity(nc, ident[:])
+
         for q in range(4):
-            nc.scalar.dma_start(
+            nc.sync.dma_start(
                 out=scale_table[32 * q : 32 * q + 4, :].bitcast(I32),
                 in_=w_scales[0, 4 * q : 4 * q + 4, :].bitcast(I32),
             )
-        nc.scalar.dma_start(out=ts_table[0:1, :], in_=ts[0:1, :])
-        wt_rows = keep.tile([P, B, PACK], F32, name="wt_rows")
-        nc.scalar.dma_start(out=wt_rows[:], in_=wt.rearrange("b (p j) o -> p b (j o)", j=PACK))
+        wt_rows = sbuf("wt_rows", [P, B, PACK], F32)
+        nc.sync.dma_start(out=wt_rows[:], in_=wt.rearrange("b (p j) o -> p b (j o)", j=PACK))
+        warm = sbuf("warm", [P, 2], F32)
+        nc.vector.memset(warm[:, 0:1], 0.0)
+        nc.scalar.activation(out=warm[:, 1:2], in_=warm[:, 0:1], func=ACT.Sigmoid)
+        x_halves = [sbuf("x_half%d" % k, [P, PACK, R // 2], F32) for k in range(2)]
+        x_in = xT[0].rearrange("(p j) r -> p j r", j=PACK)
+        nc.sync.dma_start(out=x_halves[0][:], in_=x_in[:, :, 0 : R // 2])
+        nc.sync.dma_start(out=ts_table[0:1, :], in_=ts[0:1, :])
+        nc.sync.dma_start(out=x_halves[1][:], in_=x_in[:, :, R // 2 : R])
+        word_table = keep.tile([P, T], I32, name="word_table", tag="fourth", align_bytes=64)
+        nc.sync.dma_start(out=word_table[:], in_=w_words[0].rearrange("p t j -> p (t j)").bitcast(I32))
 
-        x_raw, y_raw, xm_raw = [], [], []
+        x_second = sbuf("x_second", [P, PACK, R], F32)
+        y_raw = [[sbuf("y_raw%d_%d" % (b, k), [P, PACK, N // 2], F32) for k in range(2)] for b in range(B)]
+        xm_raw = [sbuf("xm_raw%d" % b, [P, PACK, D], F32) for b in range(B)]
         for b in range(B):
-            x_raw.append(keep.tile([P, PACK, R], F32, name="x_raw%d" % b))
-            y_raw.append(keep.tile([P, PACK, N], F32, name="y_raw%d" % b))
-            xm_raw.append(keep.tile([P, PACK, D], F32, name="xm_raw%d" % b))
-            nc.sync.dma_start(out=x_raw[b][:], in_=xT[b].rearrange("(p j) r -> p j r", j=PACK))
-            nc.sync.dma_start(out=y_raw[b][:], in_=y[b].rearrange("(c p) i -> p c i", p=P))
+            if b == 1:
+                nc.sync.dma_start(out=x_second[:], in_=xT[b].rearrange("(p j) r -> p j r", j=PACK))
+            y_in = y[b].rearrange("(c p) i -> p c i", p=P)
+            for k in range(2):
+                nc.sync.dma_start(out=y_raw[b][k][:], in_=y_in[:, :, k * N // 2 : (k + 1) * N // 2])
             nc.sync.dma_start(out=xm_raw[b][:], in_=xm[b].rearrange("(p j) d -> p j d", j=PACK))
 
-        ident = keep.tile([P, P], F32, name="ident")
-        make_identity(nc, ident[:])
-        warm = keep.tile([P, 1], F32, name="warm")
-        nc.scalar.activation(out=warm[:], in_=ident[:, 0:1], func=ACT.Sigmoid)
+        banks = [psum.tile([P, N], F32, name="bank%d" % k) for k in range(8)]
+        windows = {k: sbuf("window%d" % k, [P, T], F32) for k in (0, 1)}
 
-        windows = [keep.tile([P, T], F32, name="window%d" % k) for k in range(3)]
+        def mx_tiles(name, width):
+            return sbuf(name + "_codes", [P, width], U32), sbuf(name + "_scales", [P, width], U8)
+
+        w_codes = [sbuf("w_codes%d" % b, [P, N], U32) for b in range(B)]
+        w_bytes = [sbuf("w_bytes%d" % b, [P, N], U8) for b in range(B)]
+        x_mx = [mx_tiles("x%d" % b, R) for b in range(B)]
+        xm_mx = [mx_tiles("xm%d" % b, D) for b in range(B)]
+        h_mx = [mx_tiles("h%d" % b, N) for b in range(B)]
+        ts_second = sbuf("ts_second", [P, NB], F32)
+        ts_col = [x_halves[1][:, 0, P : P + NB], ts_second[:]]
+        h_store = [sbuf("h_store%d" % b, [P, 2 * N], F32) for b in range(B)]
+        dw = [[sbuf("dw%d_%d" % (b, k), [P, N], F32)[:] for k in range(DB)] for b in range(B)]
+        dw[0][1] = x_second[:, 0, :]
+        diff = [sbuf("diff%d" % c, [P, R], F32) for c in range(NB)]
+        h_all = sbuf("h_all", [P, 2 * R], F32)
+        h_t = [h_all[:, c * 2 * P : (c + 1) * 2 * P] for c in range(NB)]
+        sig = [sbuf("sig%d" % b, [P, NB * R], F32) for b in range(B)]
+
+        def grouped_view(tile, half):
+            return tile[:, half * 2 * R : (half + 1) * 2 * R].bitcast(BF16).rearrange("p (w t) -> p w t", t=PACK)
+
+        x_first = sbuf("x_first", [P, 2 * R], F32)
+        ts_first = sbuf("ts_first", [P, N], F32)
+        ts_listed = [ts_first[:], h_store[0][:, N : 2 * N]]
+        h_grp = [grouped_view(h_store[b], 0) for b in range(B)]
+        x_grp = [grouped_view(x_first, 0), grouped_view(x_first, 0)]
+        xm_grp = [grouped_view(sig[0], 0), grouped_view(sig[1], 0)]
 
         def interleave(engine_copy, grouped, raw, c0, c1):
             engine_copy(
                 out=grouped[:, c0:c1, :].rearrange("p (c i) t -> p c t i", i=4),
                 in_=raw[:, :, c0:c1].rearrange("p t (c i) -> p c t i", i=4),
             )
-
-        def mx_tiles(name, width):
-            codes = keep.tile([P, width], U32, name=name + "_codes", align_bytes=64)
-            scales = keep.tile([P, width], U8, name=name + "_scales", align_bytes=64)
-            return codes, scales
 
         def quantize(pair, grouped, fmt, c0, c1):
             nc.vector.quantize_mx(
@@ -87,136 +119,132 @@ def tile_attend_gnce_w_ts_kernel(tc, xT, w_words, w_scales, y, wt, ts, xm, offs,
                 in_=grouped[:, c0:c1, :].rearrange("p w t -> p (w t)"),
             )
 
-        w_mx = [mx_tiles("w%d" % b, N) for b in range(B)]
-        x_mx = [mx_tiles("x%d" % b, R) for b in range(B)]
-        xm_mx = [mx_tiles("xm%d" % b, D) for b in range(B)]
-        h_mx = [mx_tiles("h%d" % b, N) for b in range(B)]
-        ts_listed = [keep.tile([P, N], F32, name="ts_listed%d" % b) for b in range(B)]
-        ts_col = [keep.tile([P, NB], F32, name="ts_col%d" % b) for b in range(B)]
-        wt_wide = [keep.tile([P, R], F32, name="wt_wide%d" % b) for b in range(B)]
-        x_grp = [keep.tile([P, R, PACK], BF16, name="x_grp%d" % b, align_bytes=64) for b in range(B)]
-        xm_grp = [keep.tile([P, D, PACK], BF16, name="xm_grp%d" % b, align_bytes=64) for b in range(B)]
-        h_grp = [keep.tile([P, N, PACK], BF16, name="h_grp%d" % b, align_bytes=64) for b in range(B)]
-        dw = [[keep.tile([P, N], F32, name="dw%d_%d" % (b, k)) for k in range(DB)] for b in range(B)]
-
         def gather_scales(b):
-            nc.vector.tensor_copy(out=w_mx[b][1][:], in_=scale_table[:].indirect(listed(b)))
+            nc.vector.tensor_copy(out=w_bytes[b][:], in_=scale_table[:].indirect(listed(b)))
 
         def gather_words(b):
-            nc.vector.tensor_copy(out=w_mx[b][0][:], in_=word_table[:].bitcast(U32).indirect(listed(b)))
+            nc.vector.tensor_copy(out=w_codes[b][:], in_=word_table[:].bitcast(U32).indirect(listed(b)))
 
         def gather_ts(b):
-            nc.vector.tensor_copy(out=ts_listed[b][:], in_=ts_table[:].indirect(listed(b)))
-            bank = psum.tile([P, NB, P], F32, name="bank_out", tag="out")
+            nc.vector.tensor_copy(out=ts_listed[b], in_=ts_table[:].indirect(listed(b)))
+
+        def turn_ts(b, bank):
             for c in range(NB):
-                nc.tensor.transpose(bank[:, c, :], ts_listed[b][:, c * P : (c + 1) * P], ident[:])
-            nc.scalar.copy(out=ts_col[b][:], in_=bank[:, :, 0])
+                nc.tensor.transpose(bank[:, c * P : (c + 1) * P], ts_listed[b][:, c * P : (c + 1) * P], ident[:])
+            nc.scalar.copy(out=ts_col[b], in_=bank[:, 0:N:P])
 
-        def spread_wt(b):
-            bank = psum.tile([P, PACK, P], F32, name="bank_wt", tag="out")
+        def spread_wt(b, bank):
             for j in range(PACK):
-                nc.tensor.transpose(bank[:, j, :], wt_rows[:, b, j : j + 1].to_broadcast([P, P]), ident[:])
-            nc.scalar.copy(out=wt_wide[b][:].rearrange("m (p j) -> m p j", j=PACK), in_=bank[:].rearrange("m j p -> m p j"))
+                nc.tensor.transpose(bank[:, j * P : (j + 1) * P], wt_rows[:, b, j : j + 1].to_broadcast([P, P]), ident[:])
 
-        def scores(b, c):
+        def scores(b, c, bank):
             cols = slice(c * P, (c + 1) * P)
-            a = psum.tile([P, R], F32, name="bank_a", tag="a")
             nc.tensor.matmul_mx(
-                out=a[:], lhsT=w_mx[b][0][:, cols].bitcast(E4M3), lhsT_scale=w_mx[b][1][:, cols],
+                out=bank[:], lhsT=w_codes[b][:, cols].bitcast(E4M3), lhsT_scale=w_bytes[b][:, cols],
                 rhs=x_mx[b][0][:].bitcast(E4M3), rhs_scale=x_mx[b][1][:], start=True, stop=True,
             )
-            yt = psum.tile([P, PACK, P], F32, name="bank_y", tag="y")
+            nc.scalar.activation(
+                out=sig[b][:, c * R : (c + 1) * R], in_=bank[:], func=ACT.Sigmoid, scale=ts_col[b][:, c : c + 1]
+            )
+
+        def subtract(b, c, bank):
             for cr in range(PACK):
-                nc.tensor.transpose(yt[:, cr, :], y_raw[b][:, cr, cols], ident[:])
-            s = work.tile([P, R], F32, name="s")
-            nc.scalar.activation(out=s[:], in_=a[:], func=ACT.Sigmoid, scale=ts_col[b][:, c : c + 1])
-            diff = work.tile([P, R], F32, name="diff")
-            nc.vector.tensor_tensor(out=diff[:], in0=s[:], in1=yt[:].rearrange("m c p -> m (c p)"), op=ALU.subtract)
-            return diff
+                nc.tensor.transpose(bank[:, cr * P : (cr + 1) * P], y_raw[b][c // 2][:, cr, (c % 2) * P : (c % 2 + 1) * P], ident[:])
+            nc.vector.tensor_tensor(out=diff[c][:], in0=sig[b][:, c * R : (c + 1) * R], in1=bank[:], op=ALU.subtract)
 
-        def weigh(b, c, diff):
-            h = work.tile([P, R], BF16, name="h", align_bytes=64)
+        def weigh(b, c):
             nc.vector.scalar_tensor_tensor(
-                out=h[:], in0=diff[:], scalar=ts_col[b][:, c : c + 1], in1=wt_wide[b][:], op0=ALU.mult, op1=ALU.mult
+                out=h_t[c].bitcast(BF16).rearrange("m (p j) -> m p j", j=PACK),
+                in0=diff[c][:].rearrange("m (p j) -> m p j", j=PACK),
+                scalar=ts_col[b][:, c : c + 1],
+                in1=banks[7][:].rearrange("m (j p) -> m p j", j=PACK),
+                op0=ALU.mult,
+                op1=ALU.mult,
             )
-            return h
 
-        def turn(b, half, hs):
-            bank = psum.tile([P, 2, 2, P], F32, name="bank_h", tag="h")
-            for cc in range(2):
-                words = hs[cc][:].bitcast(F32)
-                for u in range(2):
-                    nc.tensor.transpose(bank[:, cc, u, :], words[:, u : 2 * P : 2], ident[:])
-            c0, c1 = half * 2 * P, (half + 1) * 2 * P
+        def turn(b, c, bank):
+            for u in range(2):
+                nc.tensor.transpose(bank[:, u * P : (u + 1) * P], h_t[c][:, u : 2 * P : 2], ident[:])
             nc.scalar.copy(
-                out=h_grp[b][:, c0:c1, :].bitcast(F32).rearrange("p (c i) u -> p c i u", c=2),
-                in_=bank[:].rearrange("p c u i -> p c i u"),
+                out=h_grp[b][:, c * P : (c + 1) * P, :].bitcast(F32),
+                in_=bank[:, 0 : 2 * P].rearrange("p (u i) -> p i u", u=2),
             )
 
-        def gradient(b):
-            diffs = [scores(b, 0), scores(b, 1)]
-            hs = [weigh(b, 0, diffs[0])]
-            diffs.append(scores(b, 2))
-            hs.append(weigh(b, 1, diffs[1]))
-            turn(b, 0, hs[0:2])
-            diffs.append(scores(b, 3))
-            hs.append(weigh(b, 2, diffs[2]))
-            quantize(h_mx[b], h_grp[b], E5M2, 0, 2 * P)
-            hs.append(weigh(b, 3, diffs[3]))
-            turn(b, 1, hs[2:4])
-
-        def product(b):
-            quantize(h_mx[b], h_grp[b], E5M2, 2 * P, 4 * P)
-            for k in range(DB):
-                cols = slice(k * P, (k + 1) * P)
-                acc = psum.tile([P, N], F32, name="bank_dw", tag="out")
-                nc.tensor.matmul_mx(
-                    out=acc[:], lhsT=xm_mx[b][0][:, cols].bitcast(E4M3), lhsT_scale=xm_mx[b][1][:, cols],
-                    rhs=h_mx[b][0][:].bitcast(E5M2), rhs_scale=h_mx[b][1][:], start=True, stop=True,
-                )
-                nc.scalar.copy(out=dw[b][k][:], in_=acc[:])
+        def product(b, k, bank):
+            cols = slice(k * P, (k + 1) * P)
+            nc.tensor.matmul_mx(
+                out=bank[:], lhsT=xm_mx[b][0][:, cols].bitcast(E4M3), lhsT_scale=xm_mx[b][1][:, cols],
+                rhs=h_mx[b][0][:].bitcast(E5M2), rhs_scale=h_mx[b][1][:], start=True, stop=True,
+            )
+            nc.scalar.copy(out=dw[b][k], in_=bank[:])
 
         def scatter(b, k):
-            nc.vector.tensor_copy(out=windows[k % 3][:].indirect(listed(b)), in_=dw[b][k][:])
+            nc.vector.tensor_copy(out=windows[k][:].indirect(listed(b)), in_=dw[b][k])
 
-        def store(k):
-            nc.sync.dma_start(out=out[k * P : (k + 1) * P, :], in_=windows[k % 3][:])
+        def gradient(b, a_banks, y_banks, h_banks, after_last_subtract):
+            scores(b, 0, banks[a_banks[0]])
+            scores(b, 1, banks[a_banks[1]])
+            subtract(b, 0, banks[y_banks[0]])
+            scores(b, 2, banks[a_banks[2]])
+            subtract(b, 1, banks[y_banks[1]])
+            scores(b, 3, banks[a_banks[3]])
+            weigh(b, 0)
+            turn(b, 0, banks[h_banks[0]])
+            subtract(b, 2, banks[y_banks[2]])
+            weigh(b, 1)
+            turn(b, 1, banks[h_banks[1]])
+            subtract(b, 3, banks[y_banks[3]])
+            weigh(b, 2)
+            turn(b, 2, banks[h_banks[0]])
+            weigh(b, 3)
+            turn(b, 3, banks[h_banks[1]])
+            after_last_subtract()
+            quantize(h_mx[b], h_grp[b], E5M2, 0, 2 * P)
+            quantize(h_mx[b], h_grp[b], E5M2, 2 * P, 3 * P)
+            quantize(h_mx[b], h_grp[b], E5M2, 3 * P, 4 * P)
 
-        spread_wt(0)
+        def prepare(pair, grouped, raw, first, last):
+            for c in range(first, last):
+                interleave(nc.scalar.copy, grouped, raw, c * P, (c + 1) * P)
+            quantize(pair, grouped, E4M3, first * P, last * P)
+
         gather_scales(0)
         gather_ts(0)
         gather_words(0)
-        interleave(nc.vector.tensor_copy, x_grp[0], x_raw[0], 0, 320)
-        interleave(nc.scalar.copy, x_grp[0], x_raw[0], 320, R)
-        quantize(x_mx[0], x_grp[0], E4M3, 0, R)
-        spread_wt(1)
-        interleave(nc.scalar.copy, xm_grp[0], xm_raw[0], 0, D // 2)
-        interleave(nc.scalar.copy, xm_grp[0], xm_raw[0], D // 2, D)
-        gradient(0)
-        quantize(xm_mx[0], xm_grp[0], E4M3, 0, D)
-        product(0)
+        for c in range(4):
+            half = x_grp[0][:, (c // 2) * 2 * P : (c // 2 + 1) * 2 * P, :]
+            interleave(nc.scalar.copy, half, x_halves[c // 2], (c % 2) * P, (c % 2 + 1) * P)
+        turn_ts(0, banks[5])
+        quantize(x_mx[0], x_grp[0], E4M3, 0, 2 * P)
+        quantize(x_mx[0], x_grp[0], E4M3, 2 * P, 4 * P)
+        spread_wt(0, banks[7])
+        gradient(0, (0, 1, 0, 1), (2, 3, 4, 2), (5, 6), lambda: prepare(xm_mx[0], xm_grp[0], xm_raw[0], 0, 1))
+        product(0, 0, banks[0])
         gather_scales(1)
+        spread_wt(1, banks[7])
         gather_ts(1)
+        turn_ts(1, banks[3])
         gather_words(1)
-        interleave(nc.scalar.copy, x_grp[1], x_raw[1], 0, R // 2)
-        interleave(nc.scalar.copy, x_grp[1], x_raw[1], R // 2, R)
-        quantize(x_mx[1], x_grp[1], E4M3, 0, R)
-        interleave(nc.scalar.copy, xm_grp[1], xm_raw[1], 0, D // 2)
-        interleave(nc.scalar.copy, xm_grp[1], xm_raw[1], D // 2, D)
-        for window in windows:
-            nc.vector.memset(window[:], 0.0)
-        gradient(1)
-        quantize(xm_mx[1], xm_grp[1], E4M3, 0, D)
-        product(1)
-        scatter(0, 0)
-        scatter(1, 0)
-        store(0)
-        scatter(0, 1)
-        scatter(1, 1)
-        store(1)
-        scatter(0, 2)
-        scatter(1, 2)
-        store(2)
-        scatter(0, 3)
-        scatter(1, 3)
-        store(3)
+        prepare(xm_mx[0], xm_grp[0], xm_raw[0], 1, 2)
+        prepare(x_mx[1], x_grp[1], x_second, 0, 4)
+        product(0, 1, banks[1])
+        prepare(xm_mx[0], xm_grp[0], xm_raw[0], 2, 4)
+        for k, tag in ((3, "fourth"), (2, "third")):
+            windows[k] = keep.tile([P, T], F32, name="window%d" % k, tag=tag, align_bytes=64)
+        for window in (windows[0], windows[1], windows[3], windows[2]):
+            for c0 in range(0, T, 512):
+                nc.gpsimd.memset(window[:, c0 : c0 + 512], 0.0)
+
+        def late_products():
+            product(0, 2, banks[4])
+            product(0, 3, banks[6])
+            prepare(xm_mx[1], xm_grp[1], xm_raw[1], 0, 4)
+
+        gradient(1, (5, 6, 5, 6), (4, 2, 3, 4), (5, 6), late_products)
+        for k, bank in enumerate((0, 1, 2, 3)):
+            product(1, k, banks[bank])
+        for k in range(DB):
+            scatter(0, k)
+        for k in range(DB):
+            scatter(1, k)
+            nc.sync.dma_start(out=out[k * P : (k + 1) * P, :], in_=windows[k][:])

@@ -70,7 +70,7 @@ def tile_attend_gnce_w_ts_kernel(tc, xT, w_words, w_scales, y, wt, ts, xm, offs,
         for b in range(B):
             if b == 1:
                 nc.sync.dma_start(out=x_second[:], in_=xT[b].rearrange("(p j) r -> p j r", j=PACK))
-            y_in = y[b].rearrange("(c p) i -> p c i", p=P)
+            y_in = y[b].rearrange("(c p) i -> p c i", p=P) if b == 0 else y[b].rearrange("(p j) i -> p j i", j=PACK)
             for k in range(2):
                 nc.sync.dma_start(out=y_raw[b][k][:], in_=y_in[:, :, k * N // 2 : (k + 1) * N // 2])
             nc.sync.dma_start(out=xm_raw[b][:], in_=xm[b].rearrange("(p j) d -> p j d", j=PACK))
@@ -90,7 +90,7 @@ def tile_attend_gnce_w_ts_kernel(tc, xT, w_words, w_scales, y, wt, ts, xm, offs,
         ts_col = [x_halves[1][:, 0, P : P + NB], ts_second[:]]
         h_store = [sbuf("h_store%d" % b, [P, 2 * N], F32) for b in range(B)]
         dw = [[sbuf("dw%d_%d" % (b, k), [P, N], F32)[:] for k in range(DB)] for b in range(B)]
-        dw[0][1] = x_second[:, 0, :]
+        dw[0][0] = x_second[:, 0, :]
         diff = [sbuf("diff%d" % c, [P, R], F32) for c in range(NB)]
         h_all = sbuf("h_all", [P, 2 * R], F32)
         h_t = [h_all[:, c * 2 * P : (c + 1) * 2 * P] for c in range(NB)]
@@ -104,7 +104,7 @@ def tile_attend_gnce_w_ts_kernel(tc, xT, w_words, w_scales, y, wt, ts, xm, offs,
         ts_listed = [ts_first[:], h_store[0][:, N : 2 * N]]
         h_grp = [grouped_view(h_store[b], 0) for b in range(B)]
         x_grp = [grouped_view(x_first, 0), grouped_view(x_first, 0)]
-        xm_grp = [grouped_view(sig[0], 0), grouped_view(sig[1], 0)]
+        xm_grp = [grouped_view(sig[0], 0), grouped_view(x_first, 0)]
 
         def interleave(engine_copy, grouped, raw, c0, c1):
             engine_copy(
@@ -170,6 +170,46 @@ def tile_attend_gnce_w_ts_kernel(tc, xT, w_words, w_scales, y, wt, ts, xm, offs,
                 in_=bank[:, 0 : 2 * P].rearrange("p (u i) -> p i u", u=2),
             )
 
+        neg_ts = sbuf("neg_ts", [P, NB], F32)
+        neg_y = [sbuf("neg_y%d" % c, [P, R], F32) for c in range(NB)]
+
+        dw[0][3] = neg_y[1][:]
+
+        def summed_block(c, a_bank, y_bank, q_bank):
+            cols = slice(c * P, (c + 1) * P)
+            s_block = sig[1][:, c * R : (c + 1) * R]
+            nc.tensor.matmul_mx(
+                out=a_bank[:], lhsT=w_codes[1][:, cols].bitcast(E4M3), lhsT_scale=w_bytes[1][:, cols],
+                rhs=x_mx[1][0][:].bitcast(E4M3), rhs_scale=x_mx[1][1][:], start=True, stop=True,
+            )
+            nc.scalar.activation(
+                out=s_block.rearrange("i (j p) -> i j p", j=PACK), in_=a_bank[:].rearrange("i (p j) -> i j p", j=PACK),
+                func=ACT.Sigmoid, scale=ts_col[1][:, c : c + 1],
+            )
+            nc.scalar.activation(out=diff[c][:], in_=s_block, func=ACT.Copy, scale=ts_col[1][:, c : c + 1])
+            for j in range(PACK):
+                nc.tensor.transpose(y_bank[:, j * P : (j + 1) * P], y_raw[1][c // 2][:, j, (c % 2) * P : (c % 2 + 1) * P], ident[:])
+            nc.scalar.activation(out=neg_y[c][:], in_=y_bank[:], func=ACT.Copy, scale=neg_ts[:, c : c + 1])
+            for j in range(PACK):
+                part = slice(j * P, (j + 1) * P)
+                nc.tensor.matmul(out=q_bank[:, part], lhsT=neg_y[c][:, part], rhs=ident[:], start=True, stop=False, is_transpose=True)
+                nc.tensor.matmul(out=q_bank[:, part], lhsT=diff[c][:, part], rhs=ident[:], start=False, stop=True, is_transpose=True)
+
+        def weigh_rows_on_scalar(c, q_bank):
+            for j in range(PACK):
+                part = slice(j * P, (j + 1) * P)
+                nc.scalar.activation(out=neg_y[c][:, part], in_=q_bank[:, part], func=ACT.Copy, scale=wt_rows[:, 1, j : j + 1])
+            interleave(nc.scalar.copy, h_grp[1][:, c * P : (c + 1) * P, :], neg_y[c][:].rearrange("p (j i) -> p j i", j=PACK), 0, P)
+
+        def weigh_rows_on_vector(c, q_bank):
+            cols = slice(c * P, (c + 1) * P)
+            nc.vector.tensor_tensor(
+                out=h_grp[1][:, cols, :],
+                in0=q_bank[:].rearrange("p (j i) -> p i j", j=PACK),
+                in1=wt_rows[:, 1:2, :].to_broadcast([P, P, PACK]),
+                op=ALU.mult,
+            )
+
         def product(b, k, bank):
             cols = slice(k * P, (k + 1) * P)
             nc.tensor.matmul_mx(
@@ -219,29 +259,44 @@ def tile_attend_gnce_w_ts_kernel(tc, xT, w_words, w_scales, y, wt, ts, xm, offs,
         quantize(x_mx[0], x_grp[0], E4M3, 2 * P, 4 * P)
         spread_wt(0, banks[7])
         gradient(0, (0, 1, 0, 1), (2, 3, 4, 2), (5, 6), lambda: prepare(xm_mx[0], xm_grp[0], xm_raw[0], 0, 1))
-        product(0, 0, banks[0])
         gather_scales(1)
-        spread_wt(1, banks[7])
         gather_ts(1)
         turn_ts(1, banks[3])
+        nc.scalar.mul(neg_ts[:], ts_col[1], -1.0)
         gather_words(1)
         prepare(xm_mx[0], xm_grp[0], xm_raw[0], 1, 2)
-        prepare(x_mx[1], x_grp[1], x_second, 0, 4)
-        product(0, 1, banks[1])
         prepare(xm_mx[0], xm_grp[0], xm_raw[0], 2, 4)
+        for c in range(4):
+            interleave(nc.vector.tensor_copy if c >= 2 else nc.scalar.copy, x_grp[1], x_second, c * P, (c + 1) * P)
+        quantize(x_mx[1], x_grp[1], E4M3, 0, R)
+        product(0, 0, banks[0])
+        product(0, 1, banks[1])
+        product(0, 2, banks[4])
         for k, tag in ((3, "fourth"), (2, "third")):
             windows[k] = keep.tile([P, T], F32, name="window%d" % k, tag=tag, align_bytes=64)
         for window in (windows[0], windows[1], windows[3], windows[2]):
             for c0 in range(0, T, 512):
                 nc.gpsimd.memset(window[:, c0 : c0 + 512], 0.0)
 
-        def late_products():
-            product(0, 2, banks[4])
-            product(0, 3, banks[6])
-            prepare(xm_mx[1], xm_grp[1], xm_raw[1], 0, 4)
-
-        gradient(1, (5, 6, 5, 6), (4, 2, 3, 4), (5, 6), late_products)
-        for k, bank in enumerate((0, 1, 2, 3)):
+        summed_block(0, banks[5], banks[2], banks[7])
+        summed_block(1, banks[6], banks[3], banks[0])
+        summed_block(2, banks[5], banks[2], banks[1])
+        summed_block(3, banks[6], banks[3], banks[4])
+        weigh_rows_on_scalar(0, banks[7])
+        weigh_rows_on_scalar(1, banks[0])
+        weigh_rows_on_vector(2, banks[1])
+        weigh_rows_on_vector(3, banks[4])
+        for c in range(8):
+            nc.gpsimd.tensor_scalar(
+                out=xm_grp[1][:, c * 64 : (c + 1) * 64, :],
+                in0=xm_raw[1][:, :, c * 64 : (c + 1) * 64].rearrange("p t w -> p w t"),
+                scalar1=1.0, scalar2=0.0, op0=ALU.mult, op1=ALU.add,
+            )
+        quantize(xm_mx[1], xm_grp[1], E4M3, 0, D)
+        quantize(h_mx[1], h_grp[1], E5M2, 0, 2 * P)
+        quantize(h_mx[1], h_grp[1], E5M2, 2 * P, 4 * P)
+        product(0, 3, banks[5])
+        for k, bank in enumerate((6, 2, 3, 7)):
             product(1, k, banks[bank])
         for k in range(DB):
             scatter(0, k)

@@ -256,6 +256,11 @@ def tile_attend_gnce_w_ts_kernel(tc, xT, w_words, w_scales, y, wt, ts, xm, offs,
             interleave(nc.scalar.copy, half, x_halves[c // 2], (c % 2) * P, (c % 2 + 1) * P)
         turn_ts(0, banks[5])
         quantize(x_mx[0], x_grp[0], E4M3, 0, 2 * P)
+        for k in range(7):
+            nc.tensor.matmul_mx(
+                out=banks[k % 2][:, 0 : 2 * P], lhsT=x_mx[0][0][:, 0:P].bitcast(E4M3), lhsT_scale=x_mx[0][1][:, 0:P],
+                rhs=x_mx[0][0][:, 0 : 2 * P].bitcast(E4M3), rhs_scale=x_mx[0][1][:, 0 : 2 * P], start=True, stop=True,
+            )
         quantize(x_mx[0], x_grp[0], E4M3, 2 * P, 4 * P)
         spread_wt(0, banks[7])
         gradient(0, (0, 1, 0, 1), (2, 3, 4, 2), (5, 6), lambda: prepare(xm_mx[0], xm_grp[0], xm_raw[0], 0, 1))

@@ -20,8 +20,12 @@ ACT = mybir.ActivationFunctionType
 P = 128
 PACK = 4
 LIST_COLS = N // 16
-NB = N // P
-DB = D // P
+BLOCKS = 4
+RUN = 4
+PSUM_BANKS = 8
+ZERO_COLS = 512
+CAST_COLS = 64
+WARM_PASSES = 7
 
 
 def tile_attend_gnce_w_ts_kernel(tc, xT, w_words, w_scales, y, wt, ts, xm, offs, out):
@@ -30,8 +34,11 @@ def tile_attend_gnce_w_ts_kernel(tc, xT, w_words, w_scales, y, wt, ts, xm, offs,
         keep = ctx.enter_context(tc.tile_pool(name="keep", bufs=1))
         psum = ctx.enter_context(tc.psum_pool(name="psum", bufs=1))
 
-        def sbuf(name, shape, dtype):
-            return keep.tile(shape, dtype, name=name, align_bytes=64)
+        def sbuf(name, shape, dtype, tag=None):
+            return keep.tile(shape, dtype, name=name, tag=tag or name, align_bytes=64)
+
+        def block(c):
+            return slice(c * P, (c + 1) * P)
 
         offsets = keep.tile([P, B * LIST_COLS], U16, name="offsets")
         nc.sync.dma_start(offsets[:], offs)
@@ -41,7 +48,7 @@ def tile_attend_gnce_w_ts_kernel(tc, xT, w_words, w_scales, y, wt, ts, xm, offs,
 
         scale_table = sbuf("scale_table", [P, T], U8)
         nc.gpsimd.memset(scale_table[:].bitcast(I32), 0)
-        ts_table = keep.tile([P, T], F32, name="ts_table", tag="third", align_bytes=64)
+        ts_table = sbuf("ts_table", [P, T], F32, tag="ts_then_window")
         nc.vector.memset(ts_table[:], 0.0)
         ident = sbuf("ident", [P, P], F32)
         make_identity(nc, ident[:])
@@ -56,26 +63,29 @@ def tile_attend_gnce_w_ts_kernel(tc, xT, w_words, w_scales, y, wt, ts, xm, offs,
         warm = sbuf("warm", [P, 2], F32)
         nc.vector.memset(warm[:, 0:1], 0.0)
         nc.scalar.activation(out=warm[:, 1:2], in_=warm[:, 0:1], func=ACT.Sigmoid)
-        x_halves = [sbuf("x_half%d" % k, [P, PACK, R // 2], F32) for k in range(2)]
-        x_in = xT[0].rearrange("(p j) r -> p j r", j=PACK)
-        nc.sync.dma_start(out=x_halves[0][:], in_=x_in[:, :, 0 : R // 2])
+
+        x0_halves = [sbuf("x0_half%d" % k, [P, PACK, R // 2], F32) for k in range(2)]
+        x0_in = xT[0].rearrange("(p j) r -> p j r", j=PACK)
+        nc.sync.dma_start(out=x0_halves[0][:], in_=x0_in[:, :, 0 : R // 2])
         nc.sync.dma_start(out=ts_table[0:1, :], in_=ts[0:1, :])
-        nc.sync.dma_start(out=x_halves[1][:], in_=x_in[:, :, R // 2 : R])
-        word_table = keep.tile([P, T], I32, name="word_table", tag="fourth", align_bytes=64)
+        nc.sync.dma_start(out=x0_halves[1][:], in_=x0_in[:, :, R // 2 : R])
+        word_table = sbuf("word_table", [P, T], I32, tag="words_then_window")
         nc.sync.dma_start(out=word_table[:], in_=w_words[0].rearrange("p t j -> p (t j)").bitcast(I32))
 
-        x_second = sbuf("x_second", [P, PACK, R], F32)
-        y_raw = [[sbuf("y_raw%d_%d" % (b, k), [P, PACK, N // 2], F32) for k in range(2)] for b in range(B)]
+        x1_raw = sbuf("x1_raw", [P, PACK, R], F32)
+        y_halves = [[sbuf("y%d_half%d" % (b, k), [P, PACK, N // 2], F32) for k in range(2)] for b in range(B)]
         xm_raw = [sbuf("xm_raw%d" % b, [P, PACK, D], F32) for b in range(B)]
-        for b in range(B):
-            if b == 1:
-                nc.sync.dma_start(out=x_second[:], in_=xT[b].rearrange("(p j) r -> p j r", j=PACK))
-            y_in = y[b].rearrange("(c p) i -> p c i", p=P) if b == 0 else y[b].rearrange("(p j) i -> p j i", j=PACK)
+
+        def load_y_and_xm(b, y_in):
             for k in range(2):
-                nc.sync.dma_start(out=y_raw[b][k][:], in_=y_in[:, :, k * N // 2 : (k + 1) * N // 2])
+                nc.sync.dma_start(out=y_halves[b][k][:], in_=y_in[:, :, k * N // 2 : (k + 1) * N // 2])
             nc.sync.dma_start(out=xm_raw[b][:], in_=xm[b].rearrange("(p j) d -> p j d", j=PACK))
 
-        banks = [psum.tile([P, N], F32, name="bank%d" % k) for k in range(8)]
+        load_y_and_xm(0, y[0].rearrange("(j p) i -> p j i", p=P))
+        nc.sync.dma_start(out=x1_raw[:], in_=xT[1].rearrange("(p j) r -> p j r", j=PACK))
+        load_y_and_xm(1, y[1].rearrange("(p j) i -> p j i", j=PACK))
+
+        banks = [psum.tile([P, N], F32, name="bank%d" % k) for k in range(PSUM_BANKS)]
         windows = {k: sbuf("window%d" % k, [P, T], F32) for k in (0, 1)}
 
         def mx_tiles(name, width):
@@ -86,37 +96,40 @@ def tile_attend_gnce_w_ts_kernel(tc, xT, w_words, w_scales, y, wt, ts, xm, offs,
         x_mx = [mx_tiles("x%d" % b, R) for b in range(B)]
         xm_mx = [mx_tiles("xm%d" % b, D) for b in range(B)]
         h_mx = [mx_tiles("h%d" % b, N) for b in range(B)]
-        ts_second = sbuf("ts_second", [P, NB], F32)
-        ts_col = [x_halves[1][:, 0, P : P + NB], ts_second[:]]
+        ts1_col = sbuf("ts1_col", [P, BLOCKS], F32)
         h_store = [sbuf("h_store%d" % b, [P, 2 * N], F32) for b in range(B)]
-        dw = [[sbuf("dw%d_%d" % (b, k), [P, N], F32)[:] for k in range(DB)] for b in range(B)]
-        dw[0][0] = x_second[:, 0, :]
-        diff = [sbuf("diff%d" % c, [P, R], F32) for c in range(NB)]
-        h_all = sbuf("h_all", [P, 2 * R], F32)
-        h_t = [h_all[:, c * 2 * P : (c + 1) * 2 * P] for c in range(NB)]
-        sig = [sbuf("sig%d" % b, [P, NB * R], F32) for b in range(B)]
+        dw0_own = {k: sbuf("dw0_%d" % k, [P, N], F32) for k in (1, 2)}
+        dw1 = [sbuf("dw1_%d" % k, [P, N], F32) for k in range(BLOCKS)]
+        mid = [sbuf("mid%d" % c, [P, R], F32) for c in range(BLOCKS)]
+        h0_words = sbuf("h0_words", [P, BLOCKS, R // 2], F32)
+        sig = [sbuf("sig%d" % b, [P, BLOCKS * R], F32) for b in range(B)]
+        x_store = sbuf("x_store", [P, 2 * R], F32)
+        ts0_listed = sbuf("ts0_listed", [P, N], F32)
+        neg_ts = sbuf("neg_ts", [P, BLOCKS], F32)
+        neg_y = [sbuf("neg_y%d" % c, [P, R], F32) for c in range(BLOCKS)]
 
-        def grouped_view(tile, half):
-            return tile[:, half * 2 * R : (half + 1) * 2 * R].bitcast(BF16).rearrange("p (w t) -> p w t", t=PACK)
+        def grouped_view(tile):
+            return tile[:, 0 : 2 * R].bitcast(BF16).rearrange("p (w t) -> p w t", t=PACK)
 
-        x_first = sbuf("x_first", [P, 2 * R], F32)
-        ts_first = sbuf("ts_first", [P, N], F32)
-        ts_listed = [ts_first[:], h_store[0][:, N : 2 * N]]
-        h_grp = [grouped_view(h_store[b], 0) for b in range(B)]
-        x_grp = [grouped_view(x_first, 0), grouped_view(x_first, 0)]
-        xm_grp = [grouped_view(sig[0], 0), grouped_view(x_first, 0)]
+        h_grp = [grouped_view(h_store[b]) for b in range(B)]
+        x_grp = grouped_view(x_store)
+        xm_grp = [grouped_view(sig[0]), x_grp]
+        ts_col = [x0_halves[1][:, 0, P : P + BLOCKS], ts1_col[:]]
+        ts_listed = [ts0_listed[:], h_store[0][:, N : 2 * N]]
+        dw = [[x1_raw[:, 0, :], dw0_own[1][:], dw0_own[2][:], neg_y[1][:]], [tile[:] for tile in dw1]]
 
         def interleave(engine_copy, grouped, raw, c0, c1):
             engine_copy(
-                out=grouped[:, c0:c1, :].rearrange("p (c i) t -> p c t i", i=4),
-                in_=raw[:, :, c0:c1].rearrange("p t (c i) -> p c t i", i=4),
+                out=grouped[:, c0:c1, :].rearrange("p (c i) t -> p c t i", i=RUN),
+                in_=raw[:, :, c0:c1].rearrange("p t (c i) -> p c t i", i=RUN),
             )
 
-        def quantize(pair, grouped, fmt, c0, c1):
+        def quantize(pair, grouped, fmt, first, last):
+            cols = slice(first * P, last * P)
             nc.vector.quantize_mx(
-                out=pair[0][:, c0:c1].bitcast(fmt),
-                scales=pair[1][:, c0:c1],
-                in_=grouped[:, c0:c1, :].rearrange("p w t -> p (w t)"),
+                out=pair[0][:, cols].bitcast(fmt),
+                scales=pair[1][:, cols],
+                in_=grouped[:, cols, :].rearrange("p w t -> p (w t)"),
             )
 
         def gather_scales(b):
@@ -129,91 +142,28 @@ def tile_attend_gnce_w_ts_kernel(tc, xT, w_words, w_scales, y, wt, ts, xm, offs,
             nc.vector.tensor_copy(out=ts_listed[b], in_=ts_table[:].indirect(listed(b)))
 
         def turn_ts(b, bank):
-            for c in range(NB):
-                nc.tensor.transpose(bank[:, c * P : (c + 1) * P], ts_listed[b][:, c * P : (c + 1) * P], ident[:])
+            for c in range(BLOCKS):
+                nc.tensor.transpose(bank[:, block(c)], ts_listed[b][:, block(c)], ident[:])
             nc.scalar.copy(out=ts_col[b], in_=bank[:, 0:N:P])
 
-        def spread_wt(b, bank):
-            for j in range(PACK):
-                nc.tensor.transpose(bank[:, j * P : (j + 1) * P], wt_rows[:, b, j : j + 1].to_broadcast([P, P]), ident[:])
-
-        def scores(b, c, bank):
-            cols = slice(c * P, (c + 1) * P)
+        def score_matmul(b, c, bank):
             nc.tensor.matmul_mx(
-                out=bank[:], lhsT=w_codes[b][:, cols].bitcast(E4M3), lhsT_scale=w_bytes[b][:, cols],
+                out=bank[:], lhsT=w_codes[b][:, block(c)].bitcast(E4M3), lhsT_scale=w_bytes[b][:, block(c)],
                 rhs=x_mx[b][0][:].bitcast(E4M3), rhs_scale=x_mx[b][1][:], start=True, stop=True,
             )
-            nc.scalar.activation(
-                out=sig[b][:, c * R : (c + 1) * R], in_=bank[:], func=ACT.Sigmoid, scale=ts_col[b][:, c : c + 1]
-            )
 
-        def subtract(b, c, bank):
-            for cr in range(PACK):
-                nc.tensor.transpose(bank[:, cr * P : (cr + 1) * P], y_raw[b][c // 2][:, cr, (c % 2) * P : (c % 2 + 1) * P], ident[:])
-            nc.vector.tensor_tensor(out=diff[c][:], in0=sig[b][:, c * R : (c + 1) * R], in1=bank[:], op=ALU.subtract)
-
-        def weigh(b, c):
-            nc.vector.scalar_tensor_tensor(
-                out=h_t[c].bitcast(BF16).rearrange("m (p j) -> m p j", j=PACK),
-                in0=diff[c][:].rearrange("m (p j) -> m p j", j=PACK),
-                scalar=ts_col[b][:, c : c + 1],
-                in1=banks[7][:].rearrange("m (j p) -> m p j", j=PACK),
-                op0=ALU.mult,
-                op1=ALU.mult,
-            )
-
-        def turn(b, c, bank):
-            for u in range(2):
-                nc.tensor.transpose(bank[:, u * P : (u + 1) * P], h_t[c][:, u : 2 * P : 2], ident[:])
-            nc.scalar.copy(
-                out=h_grp[b][:, c * P : (c + 1) * P, :].bitcast(F32),
-                in_=bank[:, 0 : 2 * P].rearrange("p (u i) -> p i u", u=2),
-            )
-
-        neg_ts = sbuf("neg_ts", [P, NB], F32)
-        neg_y = [sbuf("neg_y%d" % c, [P, R], F32) for c in range(NB)]
-
-        dw[0][3] = neg_y[1][:]
-
-        def summed_block(c, a_bank, y_bank, q_bank):
-            cols = slice(c * P, (c + 1) * P)
-            s_block = sig[1][:, c * R : (c + 1) * R]
-            nc.tensor.matmul_mx(
-                out=a_bank[:], lhsT=w_codes[1][:, cols].bitcast(E4M3), lhsT_scale=w_bytes[1][:, cols],
-                rhs=x_mx[1][0][:].bitcast(E4M3), rhs_scale=x_mx[1][1][:], start=True, stop=True,
-            )
-            nc.scalar.activation(
-                out=s_block.rearrange("i (j p) -> i j p", j=PACK), in_=a_bank[:].rearrange("i (p j) -> i j p", j=PACK),
-                func=ACT.Sigmoid, scale=ts_col[1][:, c : c + 1],
-            )
-            nc.scalar.activation(out=diff[c][:], in_=s_block, func=ACT.Copy, scale=ts_col[1][:, c : c + 1])
+        def turn_y(b, c, bank):
             for j in range(PACK):
-                nc.tensor.transpose(y_bank[:, j * P : (j + 1) * P], y_raw[1][c // 2][:, j, (c % 2) * P : (c % 2 + 1) * P], ident[:])
-            nc.scalar.activation(out=neg_y[c][:], in_=y_bank[:], func=ACT.Copy, scale=neg_ts[:, c : c + 1])
-            for j in range(PACK):
-                part = slice(j * P, (j + 1) * P)
-                nc.tensor.matmul(out=q_bank[:, part], lhsT=neg_y[c][:, part], rhs=ident[:], start=True, stop=False, is_transpose=True)
-                nc.tensor.matmul(out=q_bank[:, part], lhsT=diff[c][:, part], rhs=ident[:], start=False, stop=True, is_transpose=True)
+                nc.tensor.transpose(bank[:, block(j)], y_halves[b][c // 2][:, j, block(c % 2)], ident[:])
 
-        def weigh_rows_on_scalar(c, q_bank):
-            for j in range(PACK):
-                part = slice(j * P, (j + 1) * P)
-                nc.scalar.activation(out=neg_y[c][:, part], in_=q_bank[:, part], func=ACT.Copy, scale=wt_rows[:, 1, j : j + 1])
-            interleave(nc.scalar.copy, h_grp[1][:, c * P : (c + 1) * P, :], neg_y[c][:].rearrange("p (j i) -> p j i", j=PACK), 0, P)
-
-        def weigh_rows_on_vector(c, q_bank):
-            cols = slice(c * P, (c + 1) * P)
-            nc.vector.tensor_tensor(
-                out=h_grp[1][:, cols, :],
-                in0=q_bank[:].rearrange("p (j i) -> p i j", j=PACK),
-                in1=wt_rows[:, 1:2, :].to_broadcast([P, P, PACK]),
-                op=ALU.mult,
-            )
+        def prepare_xm0(first, last):
+            for c in range(first, last):
+                interleave(nc.scalar.copy, xm_grp[0], xm_raw[0], c * P, (c + 1) * P)
+            quantize(xm_mx[0], xm_grp[0], E4M3, first, last)
 
         def product(b, k, bank):
-            cols = slice(k * P, (k + 1) * P)
             nc.tensor.matmul_mx(
-                out=bank[:], lhsT=xm_mx[b][0][:, cols].bitcast(E4M3), lhsT_scale=xm_mx[b][1][:, cols],
+                out=bank[:], lhsT=xm_mx[b][0][:, block(k)].bitcast(E4M3), lhsT_scale=xm_mx[b][1][:, block(k)],
                 rhs=h_mx[b][0][:].bitcast(E5M2), rhs_scale=h_mx[b][1][:], start=True, stop=True,
             )
             nc.scalar.copy(out=dw[b][k], in_=bank[:])
@@ -221,90 +171,146 @@ def tile_attend_gnce_w_ts_kernel(tc, xT, w_words, w_scales, y, wt, ts, xm, offs,
         def scatter(b, k):
             nc.vector.tensor_copy(out=windows[k][:].indirect(listed(b)), in_=dw[b][k])
 
-        def gradient(b, a_banks, y_banks, h_banks, after_last_subtract):
-            scores(b, 0, banks[a_banks[0]])
-            scores(b, 1, banks[a_banks[1]])
-            subtract(b, 0, banks[y_banks[0]])
-            scores(b, 2, banks[a_banks[2]])
-            subtract(b, 1, banks[y_banks[1]])
-            scores(b, 3, banks[a_banks[3]])
-            weigh(b, 0)
-            turn(b, 0, banks[h_banks[0]])
-            subtract(b, 2, banks[y_banks[2]])
-            weigh(b, 1)
-            turn(b, 1, banks[h_banks[1]])
-            subtract(b, 3, banks[y_banks[3]])
-            weigh(b, 2)
-            turn(b, 2, banks[h_banks[0]])
-            weigh(b, 3)
-            turn(b, 3, banks[h_banks[1]])
-            after_last_subtract()
-            quantize(h_mx[b], h_grp[b], E5M2, 0, 2 * P)
-            quantize(h_mx[b], h_grp[b], E5M2, 2 * P, 3 * P)
-            quantize(h_mx[b], h_grp[b], E5M2, 3 * P, 4 * P)
+        wt_bank = banks[7]
 
-        def prepare(pair, grouped, raw, first, last):
-            for c in range(first, last):
-                interleave(nc.scalar.copy, grouped, raw, c * P, (c + 1) * P)
-            quantize(pair, grouped, E4M3, first * P, last * P)
+        def scores0(c):
+            score_matmul(0, c, banks[c % 2])
+            nc.scalar.activation(
+                out=sig[0][:, c * R : (c + 1) * R], in_=banks[c % 2][:], func=ACT.Sigmoid, scale=ts_col[0][:, c : c + 1]
+            )
+
+        def subtract0(c):
+            bank = banks[2 + c % 3]
+            turn_y(0, c, bank)
+            nc.vector.tensor_tensor(out=mid[c][:], in0=sig[0][:, c * R : (c + 1) * R], in1=bank[:], op=ALU.subtract)
+
+        def weigh_and_turn0(c):
+            nc.vector.scalar_tensor_tensor(
+                out=h0_words[:, c, :].bitcast(BF16).rearrange("m (p j) -> m p j", j=PACK),
+                in0=mid[c][:].rearrange("m (p j) -> m p j", j=PACK),
+                scalar=ts_col[0][:, c : c + 1],
+                in1=wt_bank[:].rearrange("m (j p) -> m p j", j=PACK),
+                op0=ALU.mult,
+                op1=ALU.mult,
+            )
+            bank = banks[5 + c % 2]
+            for u in range(2):
+                nc.tensor.transpose(bank[:, block(u)], h0_words[:, c, u : 2 * P : 2], ident[:])
+            nc.scalar.copy(
+                out=h_grp[0][:, block(c), :].bitcast(F32),
+                in_=bank[:, 0 : 2 * P].rearrange("p (u i) -> p i u", u=2),
+            )
+
+        sum_banks = [banks[7], banks[0], banks[1], banks[4]]
+
+        def summed_block1(c):
+            score_bank, y_bank = banks[5 + c % 2], banks[2 + c % 2]
+            sigmoids = sig[1][:, c * R : (c + 1) * R]
+            score_matmul(1, c, score_bank)
+            nc.scalar.activation(
+                out=sigmoids.rearrange("i (j p) -> i j p", j=PACK),
+                in_=score_bank[:].rearrange("i (p j) -> i j p", j=PACK),
+                func=ACT.Sigmoid,
+                scale=ts_col[1][:, c : c + 1],
+            )
+            nc.scalar.activation(out=mid[c][:], in_=sigmoids, func=ACT.Copy, scale=ts_col[1][:, c : c + 1])
+            turn_y(1, c, y_bank)
+            nc.scalar.activation(out=neg_y[c][:], in_=y_bank[:], func=ACT.Copy, scale=neg_ts[:, c : c + 1])
+            for j in range(PACK):
+                for term, first in ((neg_y[c], True), (mid[c], False)):
+                    nc.tensor.matmul(
+                        out=sum_banks[c][:, block(j)], lhsT=term[:, block(j)], rhs=ident[:],
+                        start=first, stop=not first, is_transpose=True,
+                    )
+
+        def weigh1_on_scalar(c):
+            for j in range(PACK):
+                nc.scalar.activation(
+                    out=neg_y[c][:, block(j)], in_=sum_banks[c][:, block(j)], func=ACT.Copy, scale=wt_rows[:, 1, j : j + 1]
+                )
+            interleave(nc.scalar.copy, h_grp[1][:, block(c), :], neg_y[c][:].rearrange("p (j i) -> p j i", j=PACK), 0, P)
+
+        def weigh1_on_vector(c):
+            nc.vector.tensor_tensor(
+                out=h_grp[1][:, block(c), :],
+                in0=sum_banks[c][:].rearrange("p (j i) -> p i j", j=PACK),
+                in1=wt_rows[:, 1:2, :].to_broadcast([P, P, PACK]),
+                op=ALU.mult,
+            )
 
         gather_scales(0)
         gather_ts(0)
         gather_words(0)
-        for c in range(4):
-            half = x_grp[0][:, (c // 2) * 2 * P : (c // 2 + 1) * 2 * P, :]
-            interleave(nc.scalar.copy, half, x_halves[c // 2], (c % 2) * P, (c % 2 + 1) * P)
+        for c in range(BLOCKS):
+            half = x_grp[:, (c // 2) * 2 * P : (c // 2 + 1) * 2 * P, :]
+            interleave(nc.scalar.copy, half, x0_halves[c // 2], (c % 2) * P, (c % 2 + 1) * P)
         turn_ts(0, banks[5])
-        quantize(x_mx[0], x_grp[0], E4M3, 0, 2 * P)
-        for k in range(7):
+        quantize(x_mx[0], x_grp, E4M3, 0, 2)
+        for k in range(WARM_PASSES):
             nc.tensor.matmul_mx(
-                out=banks[k % 2][:, 0 : 2 * P], lhsT=x_mx[0][0][:, 0:P].bitcast(E4M3), lhsT_scale=x_mx[0][1][:, 0:P],
-                rhs=x_mx[0][0][:, 0 : 2 * P].bitcast(E4M3), rhs_scale=x_mx[0][1][:, 0 : 2 * P], start=True, stop=True,
+                out=banks[k % 2][:, 0 : R // 2], lhsT=x_mx[0][0][:, block(0)].bitcast(E4M3), lhsT_scale=x_mx[0][1][:, block(0)],
+                rhs=x_mx[0][0][:, 0 : R // 2].bitcast(E4M3), rhs_scale=x_mx[0][1][:, 0 : R // 2], start=True, stop=True,
             )
-        quantize(x_mx[0], x_grp[0], E4M3, 2 * P, 4 * P)
-        spread_wt(0, banks[7])
-        gradient(0, (0, 1, 0, 1), (2, 3, 4, 2), (5, 6), lambda: prepare(xm_mx[0], xm_grp[0], xm_raw[0], 0, 1))
+        quantize(x_mx[0], x_grp, E4M3, 2, 4)
+        for j in range(PACK):
+            nc.tensor.transpose(wt_bank[:, block(j)], wt_rows[:, 0, j : j + 1].to_broadcast([P, P]), ident[:])
+        scores0(0)
+        scores0(1)
+        subtract0(0)
+        scores0(2)
+        subtract0(1)
+        scores0(3)
+        for c in range(BLOCKS):
+            weigh_and_turn0(c)
+            if c + 2 < BLOCKS:
+                subtract0(c + 2)
+        prepare_xm0(0, 1)
+        quantize(h_mx[0], h_grp[0], E5M2, 0, 2)
+        quantize(h_mx[0], h_grp[0], E5M2, 2, 3)
+        quantize(h_mx[0], h_grp[0], E5M2, 3, 4)
+
         gather_scales(1)
         gather_ts(1)
         turn_ts(1, banks[3])
         nc.scalar.mul(neg_ts[:], ts_col[1], -1.0)
         gather_words(1)
-        prepare(xm_mx[0], xm_grp[0], xm_raw[0], 1, 2)
-        prepare(xm_mx[0], xm_grp[0], xm_raw[0], 2, 4)
-        for c in range(4):
-            interleave(nc.vector.tensor_copy if c >= 2 else nc.scalar.copy, x_grp[1], x_second, c * P, (c + 1) * P)
-        quantize(x_mx[1], x_grp[1], E4M3, 0, R)
+        prepare_xm0(1, 2)
+        prepare_xm0(2, 4)
+        for c in range(BLOCKS):
+            interleave(nc.scalar.copy if c < BLOCKS // 2 else nc.vector.tensor_copy, x_grp, x1_raw, c * P, (c + 1) * P)
+        quantize(x_mx[1], x_grp, E4M3, 0, 4)
         product(0, 0, banks[0])
         product(0, 1, banks[1])
         product(0, 2, banks[4])
-        for k, tag in ((3, "fourth"), (2, "third")):
-            windows[k] = keep.tile([P, T], F32, name="window%d" % k, tag=tag, align_bytes=64)
-        for window in (windows[0], windows[1], windows[3], windows[2]):
-            for c0 in range(0, T, 512):
-                nc.gpsimd.memset(window[:, c0 : c0 + 512], 0.0)
 
-        summed_block(0, banks[5], banks[2], banks[7])
-        summed_block(1, banks[6], banks[3], banks[0])
-        summed_block(2, banks[5], banks[2], banks[1])
-        summed_block(3, banks[6], banks[3], banks[4])
-        weigh_rows_on_scalar(0, banks[7])
-        weigh_rows_on_scalar(1, banks[0])
-        weigh_rows_on_vector(2, banks[1])
-        weigh_rows_on_vector(3, banks[4])
-        for c in range(8):
+        windows[3] = sbuf("window3", [P, T], F32, tag="words_then_window")
+        windows[2] = sbuf("window2", [P, T], F32, tag="ts_then_window")
+        for k in (0, 1, 3, 2):
+            for c0 in range(0, T, ZERO_COLS):
+                nc.gpsimd.memset(windows[k][:, c0 : c0 + ZERO_COLS], 0.0)
+
+        for c in range(BLOCKS):
+            summed_block1(c)
+        for c in range(BLOCKS):
+            if c < BLOCKS // 2:
+                weigh1_on_scalar(c)
+            else:
+                weigh1_on_vector(c)
+        for c0 in range(0, D, CAST_COLS):
             nc.gpsimd.tensor_scalar(
-                out=xm_grp[1][:, c * 64 : (c + 1) * 64, :],
-                in0=xm_raw[1][:, :, c * 64 : (c + 1) * 64].rearrange("p t w -> p w t"),
+                out=xm_grp[1][:, c0 : c0 + CAST_COLS, :],
+                in0=xm_raw[1][:, :, c0 : c0 + CAST_COLS].rearrange("p t w -> p w t"),
                 scalar1=1.0, scalar2=0.0, op0=ALU.mult, op1=ALU.add,
             )
-        quantize(xm_mx[1], xm_grp[1], E4M3, 0, D)
-        quantize(h_mx[1], h_grp[1], E5M2, 0, 2 * P)
-        quantize(h_mx[1], h_grp[1], E5M2, 2 * P, 4 * P)
+        quantize(xm_mx[1], xm_grp[1], E4M3, 0, 4)
+        quantize(h_mx[1], h_grp[1], E5M2, 0, 2)
+        quantize(h_mx[1], h_grp[1], E5M2, 2, 4)
         product(0, 3, banks[5])
-        for k, bank in enumerate((6, 2, 3, 7)):
-            product(1, k, banks[bank])
-        for k in range(DB):
+        for k, bank in enumerate((banks[6], banks[2], banks[3], banks[7])):
+            product(1, k, bank)
+
+        for k in range(BLOCKS):
             scatter(0, k)
-        for k in range(DB):
+        for k in range(BLOCKS):
             scatter(1, k)
-            nc.sync.dma_start(out=out[k * P : (k + 1) * P, :], in_=windows[k][:])
+            nc.sync.dma_start(out=out[block(k), :], in_=windows[k][:])

@@ -19,104 +19,95 @@ ACT = mybir.ActivationFunctionType
 
 P = 128
 PACK = 4
-LIST_COLS = N // 16
 BLOCKS = 4
+HALF = N // 2
 RUN = 4
-PSUM_BANKS = 8
+PAIR = 2
 ZERO_COLS = 512
-CAST_COLS = 64
-WARM_PASSES = 7
+CAST_COLS = 128
 
 
 def tile_attend_gnce_w_ts_kernel(tc, xT, w_words, w_scales, y, wt, ts, xm, offs, out):
     nc = tc.nc
     with ExitStack() as ctx:
         keep = ctx.enter_context(tc.tile_pool(name="keep", bufs=1))
+        shared = ctx.enter_context(tc.tile_pool(name="shared", bufs=1))
         psum = ctx.enter_context(tc.psum_pool(name="psum", bufs=1))
 
-        def sbuf(name, shape, dtype, tag=None):
-            return keep.tile(shape, dtype, name=name, tag=tag or name, align_bytes=64)
+        def sbuf(name, shape, dtype, at=None):
+            if at is None:
+                return keep.tile(shape, dtype, name=name, align_bytes=64)
+            return shared.tile(shape, dtype, name=name, align_bytes=64, offset=at * 1024)
 
         def block(c):
             return slice(c * P, (c + 1) * P)
 
-        offsets = keep.tile([P, B * LIST_COLS], U16, name="offsets")
+        def half(k):
+            return slice(k * HALF, (k + 1) * HALF)
+
+        offsets = keep.tile([P, B * N // 16], U16, name="offsets")
         nc.sync.dma_start(offsets[:], offs)
 
-        def listed(b):
-            return offsets[:, b * LIST_COLS : (b + 1) * LIST_COLS]
+        def listed(b, first, count):
+            return offsets[:, (b * N + first) // 16 : (b * N + first + count) // 16]
 
         scale_table = sbuf("scale_table", [P, T], U8)
         nc.gpsimd.memset(scale_table[:].bitcast(I32), 0)
-        ts_table = sbuf("ts_table", [P, T], F32, tag="ts_then_window")
+        ts_table = sbuf("ts_table", [P, T], F32)
         nc.vector.memset(ts_table[:], 0.0)
+        windows = [sbuf("window%d" % k, [P, T], F32) for k in range(BLOCKS)]
         ident = sbuf("ident", [P, P], F32)
         make_identity(nc, ident[:])
 
+        wt_rows = sbuf("wt_rows", [P, B, PACK], F32)
+        nc.sync.dma_start(out=wt_rows[:], in_=wt.rearrange("b (p j) o -> p b (j o)", j=PACK))
         for q in range(4):
             nc.sync.dma_start(
                 out=scale_table[32 * q : 32 * q + 4, :].bitcast(I32),
                 in_=w_scales[0, 4 * q : 4 * q + 4, :].bitcast(I32),
             )
-        wt_rows = sbuf("wt_rows", [P, B, PACK], F32)
-        nc.sync.dma_start(out=wt_rows[:], in_=wt.rearrange("b (p j) o -> p b (j o)", j=PACK))
+
         warm = sbuf("warm", [P, 2], F32)
-        nc.vector.memset(warm[:, 0:1], 0.0)
+        nc.gpsimd.memset(warm[:, 0:1], 0.0)
         nc.scalar.activation(out=warm[:, 1:2], in_=warm[:, 0:1], func=ACT.Sigmoid)
 
-        x0_halves = [sbuf("x0_half%d" % k, [P, PACK, R // 2], F32) for k in range(2)]
-        x0_in = xT[0].rearrange("(p j) r -> p j r", j=PACK)
-        nc.sync.dma_start(out=x0_halves[0][:], in_=x0_in[:, :, 0 : R // 2])
+        def load_rows(name, rows):
+            tile = sbuf(name, [P, PACK, rows.shape[1]], F32)
+            nc.sync.dma_start(out=tile[:], in_=rows.rearrange("(p j) w -> p j w", j=PACK))
+            return tile
+
+        x_raw = [load_rows("x_raw0", xT[0])]
         nc.sync.dma_start(out=ts_table[0:1, :], in_=ts[0:1, :])
-        nc.sync.dma_start(out=x0_halves[1][:], in_=x0_in[:, :, R // 2 : R])
-        word_table = sbuf("word_table", [P, T], I32, tag="words_then_window")
+        word_table = sbuf("word_table", [P, T], I32, at=0)
         nc.sync.dma_start(out=word_table[:], in_=w_words[0].rearrange("p t j -> p (t j)").bitcast(I32))
+        y_raw = [load_rows("y_raw0", y[0])]
+        x_raw.append(load_rows("x_raw1", xT[1]))
+        xm_raw = [load_rows("xm_raw0", xm[0])]
+        y_raw.append(load_rows("y_raw1", y[1]))
+        xm_raw.append(load_rows("xm_raw1", xm[1]))
 
-        x1_raw = sbuf("x1_raw", [P, PACK, R], F32)
-        y_halves = [[sbuf("y%d_half%d" % (b, k), [P, PACK, N // 2], F32) for k in range(2)] for b in range(B)]
-        xm_raw = [sbuf("xm_raw%d" % b, [P, PACK, D], F32) for b in range(B)]
+        turn_banks = [psum.tile([P, N], F32, name="turn_bank%d" % k) for k in range(4)]
+        score_banks = [psum.tile([P, N], F32, name="score_bank%d" % k) for k in range(2)]
+        ts_banks = [psum.tile([P, N], F32, name="ts_bank%d" % b) for b in range(B)]
 
-        def load_y_and_xm(b, y_in):
-            for k in range(2):
-                nc.sync.dma_start(out=y_halves[b][k][:], in_=y_in[:, :, k * N // 2 : (k + 1) * N // 2])
-            nc.sync.dma_start(out=xm_raw[b][:], in_=xm[b].rearrange("(p j) d -> p j d", j=PACK))
+        def mx_tiles(name, width, at=None):
+            return sbuf(name + "_codes", [P, width], U32, at), sbuf(name + "_scales", [P, width], U8)
 
-        load_y_and_xm(0, y[0].rearrange("(j p) i -> p j i", p=P))
-        nc.sync.dma_start(out=x1_raw[:], in_=xT[1].rearrange("(p j) r -> p j r", j=PACK))
-        load_y_and_xm(1, y[1].rearrange("(p j) i -> p j i", j=PACK))
-
-        banks = [psum.tile([P, N], F32, name="bank%d" % k) for k in range(PSUM_BANKS)]
-        windows = {k: sbuf("window%d" % k, [P, T], F32) for k in (0, 1)}
-
-        def mx_tiles(name, width):
-            return sbuf(name + "_codes", [P, width], U32), sbuf(name + "_scales", [P, width], U8)
-
-        w_codes = [sbuf("w_codes%d" % b, [P, N], U32) for b in range(B)]
-        w_bytes = [sbuf("w_bytes%d" % b, [P, N], U8) for b in range(B)]
-        x_mx = [mx_tiles("x%d" % b, R) for b in range(B)]
-        xm_mx = [mx_tiles("xm%d" % b, D) for b in range(B)]
+        w_mx = [mx_tiles("w%d" % b, N, 8 + 2 * b) for b in range(B)]
+        x_mx = [mx_tiles("x0", R), mx_tiles("x1", R, 32)]
+        xm_mx = [[mx_tiles("xm%d_%d" % (b, k), HALF, ((12, 24), (20, 25))[b][k]) for k in range(2)] for b in range(B)]
         h_mx = [mx_tiles("h%d" % b, N) for b in range(B)]
-        ts1_col = sbuf("ts1_col", [P, BLOCKS], F32)
-        h_store = [sbuf("h_store%d" % b, [P, 2 * N], F32) for b in range(B)]
-        dw0_own = {k: sbuf("dw0_%d" % k, [P, N], F32) for k in (1, 2)}
-        dw1 = [sbuf("dw1_%d" % k, [P, N], F32) for k in range(BLOCKS)]
-        mid = [sbuf("mid%d" % c, [P, R], F32) for c in range(BLOCKS)]
-        h0_words = sbuf("h0_words", [P, BLOCKS, R // 2], F32)
-        sig = [sbuf("sig%d" % b, [P, BLOCKS * R], F32) for b in range(B)]
-        x_store = sbuf("x_store", [P, 2 * R], F32)
-        ts0_listed = sbuf("ts0_listed", [P, N], F32)
-        neg_ts = sbuf("neg_ts", [P, BLOCKS], F32)
-        neg_y = [sbuf("neg_y%d" % c, [P, R], F32) for c in range(BLOCKS)]
-
-        def grouped_view(tile):
-            return tile[:, 0 : 2 * R].bitcast(BF16).rearrange("p (w t) -> p w t", t=PACK)
-
-        h_grp = [grouped_view(h_store[b]) for b in range(B)]
-        x_grp = grouped_view(x_store)
-        xm_grp = [grouped_view(sig[0]), x_grp]
-        ts_col = [x0_halves[1][:, 0, P : P + BLOCKS], ts1_col[:]]
-        ts_listed = [ts0_listed[:], h_store[0][:, N : 2 * N]]
-        dw = [[x1_raw[:, 0, :], dw0_own[1][:], dw0_own[2][:], neg_y[1][:]], [tile[:] for tile in dw1]]
+        x_grp = [sbuf("x_grp%d" % b, [P, R, PACK], BF16, at=8 + 4 * b) for b in range(B)]
+        xm_grp = [[sbuf("xm_grp%d_%d" % (b, k), [P, HALF, PACK], BF16, 36 if b + k == 0 else None) for k in range(2)] for b in range(B)]
+        h_grp = [sbuf("h_grp0", [P, N, PACK], BF16), sbuf("h_grp1", [P, N, PACK], BF16, at=24)]
+        ts_listed = [sbuf("ts_listed%d" % b, [P, N], F32) for b in range(B)]
+        ts_col = [sbuf("ts_col0", [P, BLOCKS], F32, at=12), sbuf("ts_col1", [P, BLOCKS], F32)]
+        sig = [[sbuf("sig%d_%d" % (b, c), [P, R], F32) for c in range(BLOCKS)] for b in range(B)]
+        wy0 = sbuf("wy0", [P, PACK, N], F32, at=0)
+        wy1 = [sbuf("wy1_%d" % k, [P, PACK, HALF], F32) for k in range(2)]
+        wy = [[wy0[:, :, half(k)] for k in range(2)], [tile[:] for tile in wy1]]
+        g = [[sbuf("g%d_%d" % (b, k), [P, PACK, HALF], F32, ((32, 12), (36, 20))[b][k]) for k in range(2)] for b in range(B)]
+        dw = [[sbuf("dw%d_%d" % (b, k), [P, N], F32) for k in range(BLOCKS)] for b in range(B)]
 
         def interleave(engine_copy, grouped, raw, c0, c1):
             engine_copy(
@@ -124,193 +115,164 @@ def tile_attend_gnce_w_ts_kernel(tc, xT, w_words, w_scales, y, wt, ts, xm, offs,
                 in_=raw[:, :, c0:c1].rearrange("p t (c i) -> p c t i", i=RUN),
             )
 
-        def quantize(pair, grouped, fmt, first, last):
-            cols = slice(first * P, last * P)
+        def interleave_on_gpsimd(grouped, raw, c0, c1):
+            for first in range(c0, c1, CAST_COLS):
+                nc.gpsimd.tensor_scalar(
+                    out=grouped[:, first : first + CAST_COLS, :],
+                    in0=raw[:, :, first : first + CAST_COLS].rearrange("p t w -> p w t"),
+                    scalar1=1.0, scalar2=0.0, op0=ALU.mult, op1=ALU.add,
+                )
+
+        def quantize(pair, cols, grouped, fmt):
             nc.vector.quantize_mx(
-                out=pair[0][:, cols].bitcast(fmt),
-                scales=pair[1][:, cols],
-                in_=grouped[:, cols, :].rearrange("p w t -> p (w t)"),
+                out=pair[0][:, cols].bitcast(fmt), scales=pair[1][:, cols], in_=grouped.rearrange("p w t -> p (w t)")
             )
 
         def gather_scales(b):
-            nc.vector.tensor_copy(out=w_bytes[b][:], in_=scale_table[:].indirect(listed(b)))
+            nc.vector.tensor_copy(out=w_mx[b][1][:], in_=scale_table[:].indirect(listed(b, 0, N)))
 
-        def gather_words(b):
-            nc.vector.tensor_copy(out=w_codes[b][:], in_=word_table[:].bitcast(U32).indirect(listed(b)))
+        def gather_words(b, first, count):
+            nc.vector.tensor_copy(
+                out=w_mx[b][0][:, first : first + count], in_=word_table[:].bitcast(U32).indirect(listed(b, first, count))
+            )
 
         def gather_ts(b):
-            nc.vector.tensor_copy(out=ts_listed[b], in_=ts_table[:].indirect(listed(b)))
+            nc.scalar.activation(out=ts_listed[b][:], in_=ts_table[:].indirect(listed(b, 0, N)), func=ACT.Copy)
 
         def turn_ts(b, bank):
             for c in range(BLOCKS):
                 nc.tensor.transpose(bank[:, block(c)], ts_listed[b][:, block(c)], ident[:])
-            nc.scalar.copy(out=ts_col[b], in_=bank[:, 0:N:P])
+            nc.scalar.copy(out=ts_col[b][:], in_=bank[:, 0:N:P])
 
-        def score_matmul(b, c, bank):
+        def spread_ts(b):
+            for c in range(BLOCKS):
+                nc.tensor.transpose(ts_banks[b][:, block(c)], ts_col[b][:, c : c + 1].to_broadcast([P, P]), ident[:])
+
+        def sigmoids(b, c, bank):
             nc.tensor.matmul_mx(
-                out=bank[:], lhsT=w_codes[b][:, block(c)].bitcast(E4M3), lhsT_scale=w_bytes[b][:, block(c)],
+                out=bank[:], lhsT=w_mx[b][0][:, block(c)].bitcast(E4M3), lhsT_scale=w_mx[b][1][:, block(c)],
                 rhs=x_mx[b][0][:].bitcast(E4M3), rhs_scale=x_mx[b][1][:], start=True, stop=True,
             )
-
-        def turn_y(b, c, bank):
-            for j in range(PACK):
-                nc.tensor.transpose(bank[:, block(j)], y_halves[b][c // 2][:, j, block(c % 2)], ident[:])
-
-        def prepare_xm0(first, last):
-            for c in range(first, last):
-                interleave(nc.scalar.copy, xm_grp[0], xm_raw[0], c * P, (c + 1) * P)
-            quantize(xm_mx[0], xm_grp[0], E4M3, first, last)
-
-        def product(b, k, bank):
-            nc.tensor.matmul_mx(
-                out=bank[:], lhsT=xm_mx[b][0][:, block(k)].bitcast(E4M3), lhsT_scale=xm_mx[b][1][:, block(k)],
-                rhs=h_mx[b][0][:].bitcast(E5M2), rhs_scale=h_mx[b][1][:], start=True, stop=True,
-            )
-            nc.scalar.copy(out=dw[b][k], in_=bank[:])
-
-        def scatter(b, k):
-            nc.vector.tensor_copy(out=windows[k][:].indirect(listed(b)), in_=dw[b][k])
-
-        wt_bank = banks[7]
-
-        def scores0(c):
-            score_matmul(0, c, banks[c % 2])
             nc.scalar.activation(
-                out=sig[0][:, c * R : (c + 1) * R], in_=banks[c % 2][:], func=ACT.Sigmoid, scale=ts_col[0][:, c : c + 1]
-            )
-
-        def subtract0(c):
-            bank = banks[2 + c % 3]
-            turn_y(0, c, bank)
-            nc.vector.tensor_tensor(out=mid[c][:], in0=sig[0][:, c * R : (c + 1) * R], in1=bank[:], op=ALU.subtract)
-
-        def weigh_and_turn0(c):
-            nc.vector.scalar_tensor_tensor(
-                out=h0_words[:, c, :].bitcast(BF16).rearrange("m (p j) -> m p j", j=PACK),
-                in0=mid[c][:].rearrange("m (p j) -> m p j", j=PACK),
-                scalar=ts_col[0][:, c : c + 1],
-                in1=wt_bank[:].rearrange("m (j p) -> m p j", j=PACK),
-                op0=ALU.mult,
-                op1=ALU.mult,
-            )
-            bank = banks[5 + c % 2]
-            for u in range(2):
-                nc.tensor.transpose(bank[:, block(u)], h0_words[:, c, u : 2 * P : 2], ident[:])
-            nc.scalar.copy(
-                out=h_grp[0][:, block(c), :].bitcast(F32),
-                in_=bank[:, 0 : 2 * P].rearrange("p (u i) -> p i u", u=2),
-            )
-
-        sum_banks = [banks[7], banks[0], banks[1], banks[4]]
-
-        def summed_block1(c):
-            score_bank, y_bank = banks[5 + c % 2], banks[2 + c % 2]
-            sigmoids = sig[1][:, c * R : (c + 1) * R]
-            score_matmul(1, c, score_bank)
-            nc.scalar.activation(
-                out=sigmoids.rearrange("i (j p) -> i j p", j=PACK),
-                in_=score_bank[:].rearrange("i (p j) -> i j p", j=PACK),
+                out=sig[b][c][:].rearrange("i (j p) -> i j p", j=PACK),
+                in_=bank[:].rearrange("i (p j) -> i j p", j=PACK),
                 func=ACT.Sigmoid,
-                scale=ts_col[1][:, c : c + 1],
+                scale=ts_col[b][:, c : c + 1],
             )
-            nc.scalar.activation(out=mid[c][:], in_=sigmoids, func=ACT.Copy, scale=ts_col[1][:, c : c + 1])
-            turn_y(1, c, y_bank)
-            nc.scalar.activation(out=neg_y[c][:], in_=y_bank[:], func=ACT.Copy, scale=neg_ts[:, c : c + 1])
-            for j in range(PACK):
-                for term, first in ((neg_y[c], True), (mid[c], False)):
-                    nc.tensor.matmul(
-                        out=sum_banks[c][:, block(j)], lhsT=term[:, block(j)], rhs=ident[:],
-                        start=first, stop=not first, is_transpose=True,
-                    )
 
-        def weigh1_on_scalar(c):
+        def turned(k, j):
+            return turn_banks[2 * k + j // 2][:, half(j % 2)]
+
+        def turn_sigmoids(b, c):
             for j in range(PACK):
-                nc.scalar.activation(
-                    out=neg_y[c][:, block(j)], in_=sum_banks[c][:, block(j)], func=ACT.Copy, scale=wt_rows[:, 1, j : j + 1]
+                nc.tensor.transpose(turned(c // 2, j)[:, block(c % 2)], sig[b][c][:, block(j)], ident[:])
+
+        def weigh(b, k):
+            for j in range(PACK):
+                nc.vector.scalar_tensor_tensor(
+                    out=g[b][k][:, j, :], in0=turned(k, j), scalar=wt_rows[:, b, j : j + 1], in1=wy[b][k][:, j, :],
+                    op0=ALU.mult, op1=ALU.subtract,
                 )
-            interleave(nc.scalar.copy, h_grp[1][:, block(c), :], neg_y[c][:].rearrange("p (j i) -> p j i", j=PACK), 0, P)
 
-        def weigh1_on_vector(c):
+        def scale_and_group(b, k):
             nc.vector.tensor_tensor(
-                out=h_grp[1][:, block(c), :],
-                in0=sum_banks[c][:].rearrange("p (j i) -> p i j", j=PACK),
-                in1=wt_rows[:, 1:2, :].to_broadcast([P, P, PACK]),
+                out=h_grp[b][:, half(k), :].rearrange("p (c e) j -> p c j e", e=PAIR),
+                in0=g[b][k][:].rearrange("p j (c e) -> p c j e", e=PAIR),
+                in1=ts_banks[b][:, half(k)].rearrange("p (c e) -> p c e", e=PAIR).unsqueeze(2).to_broadcast(
+                    [P, HALF // PAIR, PACK, PAIR]
+                ),
                 op=ALU.mult,
             )
 
-        gather_scales(0)
-        gather_ts(0)
-        gather_words(0)
-        for c in range(BLOCKS):
-            half = x_grp[:, (c // 2) * 2 * P : (c // 2 + 1) * 2 * P, :]
-            interleave(nc.scalar.copy, half, x0_halves[c // 2], (c % 2) * P, (c % 2 + 1) * P)
-        turn_ts(0, banks[5])
-        quantize(x_mx[0], x_grp, E4M3, 0, 2)
-        for k in range(WARM_PASSES):
+        def product(b, k, bank, engine_copy):
             nc.tensor.matmul_mx(
-                out=banks[k % 2][:, 0 : R // 2], lhsT=x_mx[0][0][:, block(0)].bitcast(E4M3), lhsT_scale=x_mx[0][1][:, block(0)],
-                rhs=x_mx[0][0][:, 0 : R // 2].bitcast(E4M3), rhs_scale=x_mx[0][1][:, 0 : R // 2], start=True, stop=True,
+                out=bank[:], lhsT=xm_mx[b][k // 2][0][:, block(k % 2)].bitcast(E4M3), lhsT_scale=xm_mx[b][k // 2][1][:, block(k % 2)],
+                rhs=h_mx[b][0][:].bitcast(E5M2), rhs_scale=h_mx[b][1][:], start=True, stop=True,
             )
-        quantize(x_mx[0], x_grp, E4M3, 2, 4)
-        for j in range(PACK):
-            nc.tensor.transpose(wt_bank[:, block(j)], wt_rows[:, 0, j : j + 1].to_broadcast([P, P]), ident[:])
-        scores0(0)
-        scores0(1)
-        subtract0(0)
-        scores0(2)
-        subtract0(1)
-        scores0(3)
-        for c in range(BLOCKS):
-            weigh_and_turn0(c)
-            if c + 2 < BLOCKS:
-                subtract0(c + 2)
-        prepare_xm0(0, 1)
-        quantize(h_mx[0], h_grp[0], E5M2, 0, 2)
-        quantize(h_mx[0], h_grp[0], E5M2, 2, 3)
-        quantize(h_mx[0], h_grp[0], E5M2, 3, 4)
+            engine_copy(out=dw[b][k][:], in_=bank[:])
 
+        def scatter_on_vector(b, k):
+            nc.vector.tensor_copy(out=windows[k][:].indirect(listed(b, 0, N)), in_=dw[b][k][:])
+
+        def scatter_on_scalar(b, k):
+            for first in (0, HALF):
+                nc.scalar.activation(
+                    out=windows[k][:].indirect(listed(b, first, HALF)), in_=dw[b][k][:, first : first + HALF], func=ACT.Copy
+                )
+
+        def finish_h(b, k):
+            scale_and_group(b, k)
+            quantize(h_mx[b], half(k), h_grp[b][:, half(k), :], E5M2)
+
+        def prepare_xm(b, k):
+            interleave_on_gpsimd(xm_grp[b][k], xm_raw[b][:, :, half(k)], 0, HALF)
+            quantize(xm_mx[b][k], slice(0, HALF), xm_grp[b][k][:], E4M3)
+
+        gather_scales(0)
         gather_scales(1)
+        gather_ts(0)
+        turn_ts(0, turn_banks[3])
         gather_ts(1)
-        turn_ts(1, banks[3])
-        nc.scalar.mul(neg_ts[:], ts_col[1], -1.0)
-        gather_words(1)
-        prepare_xm0(1, 2)
-        prepare_xm0(2, 4)
-        for c in range(BLOCKS):
-            interleave(nc.scalar.copy if c < BLOCKS // 2 else nc.vector.tensor_copy, x_grp, x1_raw, c * P, (c + 1) * P)
-        quantize(x_mx[1], x_grp, E4M3, 0, 4)
-        product(0, 0, banks[0])
-        product(0, 1, banks[1])
-        product(0, 2, banks[4])
-
-        windows[3] = sbuf("window3", [P, T], F32, tag="words_then_window")
-        windows[2] = sbuf("window2", [P, T], F32, tag="ts_then_window")
-        for k in (0, 1, 3, 2):
+        interleave(nc.vector.tensor_copy, x_grp[0], x_raw[0], 0, R)
+        quantize(x_mx[0], slice(0, R), x_grp[0][:], E4M3)
+        for k in range(2):
+            gather_words(0, k * HALF, HALF)
+        gather_words(1, 0, N)
+        for j in range(PACK):
+            nc.vector.tensor_scalar(
+                out=wy0[:, j, :], in0=y_raw[0][:, j, :], scalar1=wt_rows[:, 0, j : j + 1], scalar2=None, op0=ALU.mult
+            )
+        for k in range(BLOCKS):
             for c0 in range(0, T, ZERO_COLS):
                 nc.gpsimd.memset(windows[k][:, c0 : c0 + ZERO_COLS], 0.0)
 
+        for c, bank in enumerate(ts_banks + score_banks):
+            sigmoids(0, c, bank)
+        turn_sigmoids(0, 0)
+        turn_sigmoids(0, 1)
+        spread_ts(0)
+        turn_sigmoids(0, 2)
+        turn_sigmoids(0, 3)
+        turn_ts(1, ts_banks[1])
+        spread_ts(1)
+        for k in range(2):
+            interleave(nc.scalar.copy, x_grp[1], x_raw[1], k * HALF, (k + 1) * HALF)
+        weigh(0, 0)
+        finish_h(0, 0)
+        quantize(x_mx[1], slice(0, R), x_grp[1][:], E4M3)
+        weigh(0, 1)
+        finish_h(0, 1)
+        prepare_xm(0, 0)
+        for k in range(2):
+            for j in range(PACK):
+                nc.gpsimd.tensor_scalar(
+                    out=wy[1][k][:, j, :], in0=y_raw[1][:, j, half(k)], scalar1=wt_rows[:, 1, j : j + 1], scalar2=0.0,
+                    op0=ALU.mult, op1=ALU.add,
+                )
         for c in range(BLOCKS):
-            summed_block1(c)
-        for c in range(BLOCKS):
-            if c < BLOCKS // 2:
-                weigh1_on_scalar(c)
-            else:
-                weigh1_on_vector(c)
-        for c0 in range(0, D, CAST_COLS):
-            nc.gpsimd.tensor_scalar(
-                out=xm_grp[1][:, c0 : c0 + CAST_COLS, :],
-                in0=xm_raw[1][:, :, c0 : c0 + CAST_COLS].rearrange("p t w -> p w t"),
-                scalar1=1.0, scalar2=0.0, op0=ALU.mult, op1=ALU.add,
-            )
-        quantize(xm_mx[1], xm_grp[1], E4M3, 0, 4)
-        quantize(h_mx[1], h_grp[1], E5M2, 0, 2)
-        quantize(h_mx[1], h_grp[1], E5M2, 2, 4)
-        product(0, 3, banks[5])
-        for k, bank in enumerate((banks[6], banks[2], banks[3], banks[7])):
-            product(1, k, bank)
+            sigmoids(1, c, score_banks[c % 2])
+            turn_sigmoids(1, c)
+        for k in range(2):
+            weigh(1, k)
+            finish_h(1, k)
 
-        for k in range(BLOCKS):
-            scatter(0, k)
-        for k in range(BLOCKS):
-            scatter(1, k)
+        def store(k):
             nc.sync.dma_start(out=out[block(k), :], in_=windows[k][:])
+
+        prepare_xm(0, 1)
+        prepare_xm(1, 0)
+        for b, k in ((0, 0), (0, 1), (1, 0), (0, 2), (1, 2)):
+            if (b, k) == (0, 2):
+                store(0)
+                product(0, 3, score_banks[0], nc.vector.tensor_copy)
+                prepare_xm(1, 1)
+                scatter_on_vector(0, 3)
+                product(1, 3, score_banks[0], nc.vector.tensor_copy)
+                product(1, 1, ts_banks[0], nc.vector.tensor_copy)
+                scatter_on_vector(1, 3)
+                store(3)
+                scatter_on_vector(1, 1)
+                store(1)
+            product(b, k, score_banks[1], nc.scalar.copy)
+            scatter_on_scalar(b, k)
+        store(2)

@@ -22,8 +22,7 @@ PACK = 4
 BLOCKS = 4
 HALF = N // 2
 RUN = 4
-PAIR = 2
-ZERO_COLS = 512
+ZERO_COLS = 1024
 CAST_COLS = 128
 
 
@@ -55,7 +54,6 @@ def tile_attend_gnce_w_ts_kernel(tc, xT, w_words, w_scales, y, wt, ts, xm, offs,
         nc.gpsimd.memset(scale_table[:].bitcast(I32), 0)
         ts_table = sbuf("ts_table", [P, T], F32)
         nc.vector.memset(ts_table[:], 0.0)
-        windows = [sbuf("window%d" % k, [P, T], F32) for k in range(BLOCKS)]
         ident = sbuf("ident", [P, P], F32)
         make_identity(nc, ident[:])
 
@@ -66,7 +64,6 @@ def tile_attend_gnce_w_ts_kernel(tc, xT, w_words, w_scales, y, wt, ts, xm, offs,
                 out=scale_table[32 * q : 32 * q + 4, :].bitcast(I32),
                 in_=w_scales[0, 4 * q : 4 * q + 4, :].bitcast(I32),
             )
-
         warm = sbuf("warm", [P, 2], F32)
         nc.gpsimd.memset(warm[:, 0:1], 0.0)
         nc.scalar.activation(out=warm[:, 1:2], in_=warm[:, 0:1], func=ACT.Sigmoid)
@@ -82,32 +79,43 @@ def tile_attend_gnce_w_ts_kernel(tc, xT, w_words, w_scales, y, wt, ts, xm, offs,
         nc.sync.dma_start(out=word_table[:], in_=w_words[0].rearrange("p t j -> p (t j)").bitcast(I32))
         y_raw = [load_rows("y_raw0", y[0])]
         x_raw.append(load_rows("x_raw1", xT[1]))
-        xm_raw = [load_rows("xm_raw0", xm[0])]
         y_raw.append(load_rows("y_raw1", y[1]))
-        xm_raw.append(load_rows("xm_raw1", xm[1]))
+        xm_raw = [load_rows("xm_raw%d" % b, xm[b]) for b in range(B)]
 
-        turn_banks = [psum.tile([P, N], F32, name="turn_bank%d" % k) for k in range(4)]
-        score_banks = [psum.tile([P, N], F32, name="score_bank%d" % k) for k in range(2)]
-        ts_banks = [psum.tile([P, N], F32, name="ts_bank%d" % b) for b in range(B)]
+        banks = [psum.tile([P, N], F32, name="bank%d" % k) for k in range(8)]
 
         def mx_tiles(name, width, at=None):
             return sbuf(name + "_codes", [P, width], U32, at), sbuf(name + "_scales", [P, width], U8)
 
-        w_mx = [mx_tiles("w%d" % b, N, 8 + 2 * b) for b in range(B)]
-        x_mx = [mx_tiles("x0", R), mx_tiles("x1", R, 32)]
-        xm_mx = [[mx_tiles("xm%d_%d" % (b, k), HALF, ((12, 24), (20, 25))[b][k]) for k in range(2)] for b in range(B)]
-        h_mx = [mx_tiles("h%d" % b, N) for b in range(B)]
-        x_grp = [sbuf("x_grp%d" % b, [P, R, PACK], BF16, at=8 + 4 * b) for b in range(B)]
-        xm_grp = [[sbuf("xm_grp%d_%d" % (b, k), [P, HALF, PACK], BF16, 36 if b + k == 0 else None) for k in range(2)] for b in range(B)]
-        h_grp = [sbuf("h_grp0", [P, N, PACK], BF16), sbuf("h_grp1", [P, N, PACK], BF16, at=24)]
+        x_grp = [sbuf("x_grp0", [P, R, PACK], BF16, at=9), sbuf("x_grp1", [P, R, PACK], BF16, at=20)]
+        w_mx = [mx_tiles("w0", N, 8), mx_tiles("w1", N, 10)]
+        windows = [
+            sbuf("window0", [P, T], F32),
+            sbuf("window1", [P, T], F32, at=0),
+            sbuf("window2", [P, T], F32, at=40),
+            sbuf("window3", [P, T], F32, at=12),
+        ]
         ts_listed = [sbuf("ts_listed%d" % b, [P, N], F32) for b in range(B)]
-        ts_col = [sbuf("ts_col0", [P, BLOCKS], F32, at=12), sbuf("ts_col1", [P, BLOCKS], F32)]
-        sig = [[sbuf("sig%d_%d" % (b, c), [P, R], F32) for c in range(BLOCKS)] for b in range(B)]
-        wy0 = sbuf("wy0", [P, PACK, N], F32, at=0)
-        wy1 = [sbuf("wy1_%d" % k, [P, PACK, HALF], F32) for k in range(2)]
-        wy = [[wy0[:, :, half(k)] for k in range(2)], [tile[:] for tile in wy1]]
-        g = [[sbuf("g%d_%d" % (b, k), [P, PACK, HALF], F32, ((32, 12), (36, 20))[b][k]) for k in range(2)] for b in range(B)]
+        ts_inner = [sbuf("ts_inner%d" % b, [P, BLOCKS], F32, at=(20, 28)[b]) for b in range(B)]
+        ts_outer = [sbuf("ts_outer%d" % b, [P, BLOCKS], F32) for b in range(B)]
+        sig = [[sbuf("sig%d_%d" % (b, c), [P, R], F32, 24 if (b, c) == (0, 3) else None) for c in range(BLOCKS)] for b in range(B)]
+        x_mx = [mx_tiles("x0", R), mx_tiles("x1", R, 24)]
+        mid = [[sbuf("mid%d_%d" % (b, c), [P, R], F32) for c in range(BLOCKS)] for b in range(B)]
+        h_words = [
+            [sbuf("h_words%d_%d" % (b, c), [P, R // 2], F32, 20 if (b, c) == (0, 2) else None) for c in range(BLOCKS)]
+            for b in range(B)
+        ]
+        h_grp = [sbuf("h_grp0", [P, N, PACK], BF16), sbuf("h_grp1", [P, N, PACK], BF16, at=32)]
+        h_mx = [mx_tiles("h%d" % b, N) for b in range(B)]
+        xm_grp = [
+            [sbuf("xm_grp%d_%d" % (b, k), [P, HALF, PACK], BF16, ((28, None), (None, 40))[b][k]) for k in range(2)]
+            for b in range(B)
+        ]
+        xm_mx = [
+            [mx_tiles("xm%d_%d" % (b, k), HALF, ((None, 34), (32, 35))[b][k]) for k in range(2)] for b in range(B)
+        ]
         dw = [[sbuf("dw%d_%d" % (b, k), [P, N], F32) for k in range(BLOCKS)] for b in range(B)]
+        wt_bank = banks[7]
 
         def interleave(engine_copy, grouped, raw, c0, c1):
             engine_copy(
@@ -115,8 +123,8 @@ def tile_attend_gnce_w_ts_kernel(tc, xT, w_words, w_scales, y, wt, ts, xm, offs,
                 in_=raw[:, :, c0:c1].rearrange("p t (c i) -> p c t i", i=RUN),
             )
 
-        def interleave_on_gpsimd(grouped, raw, c0, c1):
-            for first in range(c0, c1, CAST_COLS):
+        def interleave_on_gpsimd(grouped, raw):
+            for first in range(0, HALF, CAST_COLS):
                 nc.gpsimd.tensor_scalar(
                     out=grouped[:, first : first + CAST_COLS, :],
                     in0=raw[:, :, first : first + CAST_COLS].rearrange("p t w -> p w t"),
@@ -127,6 +135,10 @@ def tile_attend_gnce_w_ts_kernel(tc, xT, w_words, w_scales, y, wt, ts, xm, offs,
             nc.vector.quantize_mx(
                 out=pair[0][:, cols].bitcast(fmt), scales=pair[1][:, cols], in_=grouped.rearrange("p w t -> p (w t)")
             )
+
+        def zero(window):
+            for c0 in range(0, T, ZERO_COLS):
+                nc.gpsimd.memset(window[:, c0 : c0 + ZERO_COLS], 0.0)
 
         def gather_scales(b):
             nc.vector.tensor_copy(out=w_mx[b][1][:], in_=scale_table[:].indirect(listed(b, 0, N)))
@@ -142,51 +154,59 @@ def tile_attend_gnce_w_ts_kernel(tc, xT, w_words, w_scales, y, wt, ts, xm, offs,
         def turn_ts(b, bank):
             for c in range(BLOCKS):
                 nc.tensor.transpose(bank[:, block(c)], ts_listed[b][:, block(c)], ident[:])
-            nc.scalar.copy(out=ts_col[b][:], in_=bank[:, 0:N:P])
+            nc.scalar.copy(out=ts_inner[b][:], in_=bank[:, 0:N:P])
+            nc.scalar.copy(out=ts_outer[b][:], in_=bank[:, 0:N:P])
 
-        def spread_ts(b):
-            for c in range(BLOCKS):
-                nc.tensor.transpose(ts_banks[b][:, block(c)], ts_col[b][:, c : c + 1].to_broadcast([P, P]), ident[:])
+        def spread_wt(b):
+            for j in range(PACK):
+                nc.tensor.transpose(wt_bank[:, block(j)], wt_rows[:, b, j : j + 1].to_broadcast([P, P]), ident[:])
 
         def sigmoids(b, c, bank):
             nc.tensor.matmul_mx(
                 out=bank[:], lhsT=w_mx[b][0][:, block(c)].bitcast(E4M3), lhsT_scale=w_mx[b][1][:, block(c)],
                 rhs=x_mx[b][0][:].bitcast(E4M3), rhs_scale=x_mx[b][1][:], start=True, stop=True,
             )
-            nc.scalar.activation(
-                out=sig[b][c][:].rearrange("i (j p) -> i j p", j=PACK),
-                in_=bank[:].rearrange("i (p j) -> i j p", j=PACK),
-                func=ACT.Sigmoid,
-                scale=ts_col[b][:, c : c + 1],
-            )
+            nc.scalar.activation(out=sig[b][c][:], in_=bank[:], func=ACT.Sigmoid, scale=ts_inner[b][:, c : c + 1])
 
-        def turned(k, j):
-            return turn_banks[2 * k + j // 2][:, half(j % 2)]
-
-        def turn_sigmoids(b, c):
+        def turn_y(b, c, bank):
             for j in range(PACK):
-                nc.tensor.transpose(turned(c // 2, j)[:, block(c % 2)], sig[b][c][:, block(j)], ident[:])
+                nc.tensor.transpose(bank[:, block(j)], y_raw[b][:, j, block(c)], ident[:])
 
-        def weigh(b, k):
-            for j in range(PACK):
-                nc.vector.scalar_tensor_tensor(
-                    out=g[b][k][:, j, :], in0=turned(k, j), scalar=wt_rows[:, b, j : j + 1], in1=wy[b][k][:, j, :],
-                    op0=ALU.mult, op1=ALU.subtract,
-                )
-
-        def scale_and_group(b, k):
+        def subtract(b, c, bank):
             nc.vector.tensor_tensor(
-                out=h_grp[b][:, half(k), :].rearrange("p (c e) j -> p c j e", e=PAIR),
-                in0=g[b][k][:].rearrange("p j (c e) -> p c j e", e=PAIR),
-                in1=ts_banks[b][:, half(k)].rearrange("p (c e) -> p c e", e=PAIR).unsqueeze(2).to_broadcast(
-                    [P, HALF // PAIR, PACK, PAIR]
-                ),
-                op=ALU.mult,
+                out=mid[b][c][:].rearrange("i (p j) -> i p j", j=PACK),
+                in0=sig[b][c][:].rearrange("i (p j) -> i p j", j=PACK),
+                in1=bank[:].rearrange("i (j p) -> i p j", j=PACK),
+                op=ALU.subtract,
             )
+
+        def weigh(b, c):
+            nc.vector.scalar_tensor_tensor(
+                out=h_words[b][c][:].bitcast(BF16).rearrange("i (p j) -> i p j", j=PACK),
+                in0=mid[b][c][:].rearrange("i (p j) -> i p j", j=PACK),
+                scalar=ts_outer[b][:, c : c + 1],
+                in1=wt_bank[:].rearrange("i (j p) -> i p j", j=PACK),
+                op0=ALU.mult,
+                op1=ALU.mult,
+            )
+
+        def turn_h(b, c, bank, engine_copy):
+            for u in range(2):
+                nc.tensor.transpose(bank[:, block(u)], h_words[b][c][:, u : 2 * P : 2], ident[:])
+            engine_copy(
+                out=h_grp[b][:, block(c), :].bitcast(F32), in_=bank[:, 0 : 2 * P].rearrange("p (u i) -> p i u", u=2)
+            )
+
+        def quantize_h(b, k):
+            quantize(h_mx[b], half(k), h_grp[b][:, half(k), :], E5M2)
+
+        def quantize_xm(b, k):
+            quantize(xm_mx[b][k], slice(0, HALF), xm_grp[b][k][:], E4M3)
 
         def product(b, k, bank, engine_copy):
+            codes, scales = xm_mx[b][k // 2]
             nc.tensor.matmul_mx(
-                out=bank[:], lhsT=xm_mx[b][k // 2][0][:, block(k % 2)].bitcast(E4M3), lhsT_scale=xm_mx[b][k // 2][1][:, block(k % 2)],
+                out=bank[:], lhsT=codes[:, block(k % 2)].bitcast(E4M3), lhsT_scale=scales[:, block(k % 2)],
                 rhs=h_mx[b][0][:].bitcast(E5M2), rhs_scale=h_mx[b][1][:], start=True, stop=True,
             )
             engine_copy(out=dw[b][k][:], in_=bank[:])
@@ -200,79 +220,86 @@ def tile_attend_gnce_w_ts_kernel(tc, xT, w_words, w_scales, y, wt, ts, xm, offs,
                     out=windows[k][:].indirect(listed(b, first, HALF)), in_=dw[b][k][:, first : first + HALF], func=ACT.Copy
                 )
 
-        def finish_h(b, k):
-            scale_and_group(b, k)
-            quantize(h_mx[b], half(k), h_grp[b][:, half(k), :], E5M2)
+        def store(k):
+            nc.sync.dma_start(out=out[block(k), :], in_=windows[k][:])
 
-        def prepare_xm(b, k):
-            interleave_on_gpsimd(xm_grp[b][k], xm_raw[b][:, :, half(k)], 0, HALF)
-            quantize(xm_mx[b][k], slice(0, HALF), xm_grp[b][k][:], E4M3)
-
+        zero(windows[0])
         gather_scales(0)
         gather_scales(1)
         gather_ts(0)
-        turn_ts(0, turn_banks[3])
+        turn_ts(0, banks[4])
         gather_ts(1)
+        spread_wt(0)
         interleave(nc.vector.tensor_copy, x_grp[0], x_raw[0], 0, R)
         quantize(x_mx[0], slice(0, R), x_grp[0][:], E4M3)
         for k in range(2):
             gather_words(0, k * HALF, HALF)
         gather_words(1, 0, N)
-        for j in range(PACK):
-            nc.vector.tensor_scalar(
-                out=wy0[:, j, :], in0=y_raw[0][:, j, :], scalar1=wt_rows[:, 0, j : j + 1], scalar2=None, op0=ALU.mult
-            )
-        for k in range(BLOCKS):
-            for c0 in range(0, T, ZERO_COLS):
-                nc.gpsimd.memset(windows[k][:, c0 : c0 + ZERO_COLS], 0.0)
+        zero(windows[3])
+        zero(windows[1])
 
-        for c, bank in enumerate(ts_banks + score_banks):
-            sigmoids(0, c, bank)
-        turn_sigmoids(0, 0)
-        turn_sigmoids(0, 1)
-        spread_ts(0)
-        turn_sigmoids(0, 2)
-        turn_sigmoids(0, 3)
-        turn_ts(1, ts_banks[1])
-        spread_ts(1)
+        for c in range(BLOCKS):
+            sigmoids(0, c, banks[c])
+        for c in range(BLOCKS):
+            turn_y(0, c, banks[c])
         for k in range(2):
             interleave(nc.scalar.copy, x_grp[1], x_raw[1], k * HALF, (k + 1) * HALF)
+        subtract(0, 0, banks[0])
+        turn_ts(1, banks[0])
+        subtract(0, 1, banks[1])
         weigh(0, 0)
-        finish_h(0, 0)
-        quantize(x_mx[1], slice(0, R), x_grp[1][:], E4M3)
+        turn_h(0, 0, banks[4], nc.scalar.copy)
+        subtract(0, 2, banks[2])
         weigh(0, 1)
-        finish_h(0, 1)
-        prepare_xm(0, 0)
-        for k in range(2):
-            for j in range(PACK):
-                nc.gpsimd.tensor_scalar(
-                    out=wy[1][k][:, j, :], in0=y_raw[1][:, j, half(k)], scalar1=wt_rows[:, 1, j : j + 1], scalar2=0.0,
-                    op0=ALU.mult, op1=ALU.add,
-                )
-        for c in range(BLOCKS):
-            sigmoids(1, c, score_banks[c % 2])
-            turn_sigmoids(1, c)
-        for k in range(2):
-            weigh(1, k)
-            finish_h(1, k)
+        turn_h(0, 1, banks[5], nc.scalar.copy)
+        subtract(0, 3, banks[3])
+        quantize(x_mx[1], slice(0, R), x_grp[1][:], E4M3)
+        y_banks = (banks[2], banks[3], banks[1], banks[6])
+        for c in range(2):
+            turn_y(1, c, y_banks[c])
+        for c, bank in enumerate((banks[0], banks[1], banks[6], banks[0])):
+            sigmoids(1, c, bank)
+        weigh(0, 2)
+        turn_h(0, 2, banks[4], nc.scalar.copy)
+        weigh(0, 3)
+        turn_h(0, 3, banks[5], nc.scalar.copy)
+        quantize_h(0, 0)
+        quantize_h(0, 1)
 
-        def store(k):
-            nc.sync.dma_start(out=out[block(k), :], in_=windows[k][:])
+        spread_wt(1)
+        for c in range(2, BLOCKS):
+            turn_y(1, c, y_banks[c])
+        for c in range(2):
+            interleave(nc.scalar.copy, xm_grp[0][0], xm_raw[0], c * P, (c + 1) * P)
+        quantize_xm(0, 0)
+        for b, k in ((1, 0), (0, 1), (1, 1)):
+            interleave_on_gpsimd(xm_grp[b][k], xm_raw[b][:, :, half(k)])
+        subtract(1, 0, y_banks[0])
+        subtract(1, 1, y_banks[1])
+        weigh(1, 0)
+        turn_h(1, 0, banks[4], nc.scalar.copy)
+        subtract(1, 2, y_banks[2])
+        weigh(1, 1)
+        turn_h(1, 1, banks[5], nc.scalar.copy)
+        subtract(1, 3, y_banks[3])
+        weigh(1, 2)
+        turn_h(1, 2, banks[0], nc.vector.tensor_copy)
+        weigh(1, 3)
+        turn_h(1, 3, banks[2], nc.vector.tensor_copy)
+        quantize_h(1, 0)
+        quantize_h(1, 1)
+        quantize_xm(1, 0)
 
-        prepare_xm(0, 1)
-        prepare_xm(1, 0)
-        for b, k in ((0, 0), (0, 1), (1, 0), (0, 2), (1, 2)):
-            if (b, k) == (0, 2):
-                store(0)
-                product(0, 3, score_banks[0], nc.vector.tensor_copy)
-                prepare_xm(1, 1)
-                scatter_on_vector(0, 3)
-                product(1, 3, score_banks[0], nc.vector.tensor_copy)
-                product(1, 1, ts_banks[0], nc.vector.tensor_copy)
-                scatter_on_vector(1, 3)
-                store(3)
-                scatter_on_vector(1, 1)
-                store(1)
-            product(b, k, score_banks[1], nc.scalar.copy)
-            scatter_on_scalar(b, k)
-        store(2)
+        product(0, 1, banks[2], nc.vector.tensor_copy)
+        quantize_xm(0, 1)
+        quantize_xm(1, 1)
+        zero(windows[2])
+        for first in (0, 2):
+            for b in range(B):
+                product(b, first, banks[5], nc.scalar.copy)
+                scatter_on_scalar(b, first)
+                if (first, b) != (0, 0):
+                    product(b, first + 1, banks[2], nc.vector.tensor_copy)
+                scatter_on_vector(b, first + 1)
+            store(first)
+            store(first + 1)

@@ -36,7 +36,7 @@ def tile_attend_gnce_w_ts_kernel(tc, xT, w_words, w_scales, y, wt, ts, xm, offs,
         def sbuf(name, shape, dtype, at=None):
             if at is None:
                 return keep.tile(shape, dtype, name=name, align_bytes=64)
-            return shared.tile(shape, dtype, name=name, align_bytes=64, offset=at * 1024)
+            return shared.tile(shape, dtype, name=name, align_bytes=64, offset=int(at * 1024))
 
         def block(c):
             return slice(c * P, (c + 1) * P)
@@ -80,7 +80,10 @@ def tile_attend_gnce_w_ts_kernel(tc, xT, w_words, w_scales, y, wt, ts, xm, offs,
         y_raw = [load_rows("y_raw0", y[0])]
         x_raw.append(load_rows("x_raw1", xT[1]))
         y_raw.append(load_rows("y_raw1", y[1]))
-        xm_raw = [load_rows("xm_raw%d" % b, xm[b]) for b in range(B)]
+        xm0_first = load_rows("xm_raw0_0", xm[0][:, half(0)])
+        xm1_whole = load_rows("xm_raw1", xm[1])
+        xm0_second = load_rows("xm_raw0_1", xm[0][:, half(1)])
+        xm_raw = [[xm0_first[:], xm0_second[:]], [xm1_whole[:, :, half(k)] for k in range(2)]]
 
         banks = [psum.tile([P, N], F32, name="bank%d" % k) for k in range(8)]
 
@@ -96,26 +99,29 @@ def tile_attend_gnce_w_ts_kernel(tc, xT, w_words, w_scales, y, wt, ts, xm, offs,
             sbuf("window3", [P, T], F32, at=12),
         ]
         ts_listed = [sbuf("ts_listed%d" % b, [P, N], F32) for b in range(B)]
-        ts_inner = [sbuf("ts_inner%d" % b, [P, BLOCKS], F32, at=(20, 28)[b]) for b in range(B)]
+        ts_inner = [sbuf("ts_inner%d" % b, [P, 32], F32, at=(20, 50)[b])[:, 0:BLOCKS] for b in range(B)]
         ts_outer = [sbuf("ts_outer%d" % b, [P, BLOCKS], F32) for b in range(B)]
-        sig = [[sbuf("sig%d_%d" % (b, c), [P, R], F32, 24 if (b, c) == (0, 3) else None) for c in range(BLOCKS)] for b in range(B)]
+        sig = [[sbuf("sig%d_%d" % (b, c), [P, R], F32) for c in range(BLOCKS)] for b in range(B)]
         x_mx = [mx_tiles("x0", R), mx_tiles("x1", R, 24)]
-        mid = [[sbuf("mid%d_%d" % (b, c), [P, R], F32) for c in range(BLOCKS)] for b in range(B)]
+        mid = [[sbuf("mid%d_%d" % (b, c), [P, R], F32, {(0, 2): 24, (1, 1): 32, (1, 2): 28}.get((b, c))) for c in range(BLOCKS)] for b in range(B)]
         h_words = [
-            [sbuf("h_words%d_%d" % (b, c), [P, R // 2], F32, 20 if (b, c) == (0, 2) else None) for c in range(BLOCKS)]
+            [sbuf("h_words%d_%d" % (b, c), [P, R // 2], F32, {(0, 3): 20, (1, 2): 34, (1, 3): 36}.get((b, c))) for c in range(BLOCKS)]
             for b in range(B)
         ]
-        h_grp = [sbuf("h_grp0", [P, N, PACK], BF16), sbuf("h_grp1", [P, N, PACK], BF16, at=32)]
+        h_grp = [sbuf("h_grp0", [P, N, PACK], BF16), sbuf("h_grp1", [P, N, PACK], BF16)]
         h_mx = [mx_tiles("h%d" % b, N) for b in range(B)]
         xm_grp = [
             [sbuf("xm_grp%d_%d" % (b, k), [P, HALF, PACK], BF16, ((28, None), (None, 40))[b][k]) for k in range(2)]
             for b in range(B)
         ]
         xm_mx = [
-            [mx_tiles("xm%d_%d" % (b, k), HALF, ((None, 34), (32, 35))[b][k]) for k in range(2)] for b in range(B)
+            [mx_tiles("xm%d_%d" % (b, k), HALF, ((None, 28), (32, 34))[b][k]) for k in range(2)] for b in range(B)
         ]
-        dw = [[sbuf("dw%d_%d" % (b, k), [P, N], F32) for k in range(BLOCKS)] for b in range(B)]
-        wt_bank = banks[7]
+        dw = [
+            [sbuf("dw%d_%d" % (b, k), [P, N], F32, {(0, 0): 48.0625, (0, 1): 50.0625, (0, 3): 36}.get((b, k))) for k in range(BLOCKS)]
+            for b in range(B)
+        ]
+        wt_banks = (banks[7], banks[5])
 
         def interleave(engine_copy, grouped, raw, c0, c1):
             engine_copy(
@@ -154,12 +160,12 @@ def tile_attend_gnce_w_ts_kernel(tc, xT, w_words, w_scales, y, wt, ts, xm, offs,
         def turn_ts(b, bank):
             for c in range(BLOCKS):
                 nc.tensor.transpose(bank[:, block(c)], ts_listed[b][:, block(c)], ident[:])
-            nc.scalar.copy(out=ts_inner[b][:], in_=bank[:, 0:N:P])
+            nc.scalar.copy(out=ts_inner[b], in_=bank[:, 0:N:P])
             nc.scalar.copy(out=ts_outer[b][:], in_=bank[:, 0:N:P])
 
         def spread_wt(b):
             for j in range(PACK):
-                nc.tensor.transpose(wt_bank[:, block(j)], wt_rows[:, b, j : j + 1].to_broadcast([P, P]), ident[:])
+                nc.tensor.transpose(wt_banks[b][:, block(j)], wt_rows[:, b, j : j + 1].to_broadcast([P, P]), ident[:])
 
         def sigmoids(b, c, bank):
             nc.tensor.matmul_mx(
@@ -185,7 +191,7 @@ def tile_attend_gnce_w_ts_kernel(tc, xT, w_words, w_scales, y, wt, ts, xm, offs,
                 out=h_words[b][c][:].bitcast(BF16).rearrange("i (p j) -> i p j", j=PACK),
                 in0=mid[b][c][:].rearrange("i (p j) -> i p j", j=PACK),
                 scalar=ts_outer[b][:, c : c + 1],
-                in1=wt_bank[:].rearrange("i (j p) -> i p j", j=PACK),
+                in1=wt_banks[b][:].rearrange("i (j p) -> i p j", j=PACK),
                 op0=ALU.mult,
                 op1=ALU.mult,
             )
@@ -221,7 +227,7 @@ def tile_attend_gnce_w_ts_kernel(tc, xT, w_words, w_scales, y, wt, ts, xm, offs,
                 )
 
         def store(k):
-            nc.sync.dma_start(out=out[block(k), :], in_=windows[k][:])
+            (nc.scalar if k % 2 == 0 else nc.sync).dma_start(out=out[block(k), :], in_=windows[k][:])
 
         zero(windows[0])
         gather_scales(0)
@@ -230,6 +236,7 @@ def tile_attend_gnce_w_ts_kernel(tc, xT, w_words, w_scales, y, wt, ts, xm, offs,
         turn_ts(0, banks[4])
         gather_ts(1)
         spread_wt(0)
+        spread_wt(1)
         interleave(nc.vector.tensor_copy, x_grp[0], x_raw[0], 0, R)
         quantize(x_mx[0], slice(0, R), x_grp[0][:], E4M3)
         for k in range(2):
@@ -251,55 +258,62 @@ def tile_attend_gnce_w_ts_kernel(tc, xT, w_words, w_scales, y, wt, ts, xm, offs,
         turn_h(0, 0, banks[4], nc.scalar.copy)
         subtract(0, 2, banks[2])
         weigh(0, 1)
-        turn_h(0, 1, banks[5], nc.scalar.copy)
+        turn_h(0, 1, banks[4], nc.scalar.copy)
         subtract(0, 3, banks[3])
-        quantize(x_mx[1], slice(0, R), x_grp[1][:], E4M3)
-        y_banks = (banks[2], banks[3], banks[1], banks[6])
-        for c in range(2):
-            turn_y(1, c, y_banks[c])
-        for c, bank in enumerate((banks[0], banks[1], banks[6], banks[0])):
-            sigmoids(1, c, bank)
         weigh(0, 2)
         turn_h(0, 2, banks[4], nc.scalar.copy)
+        quantize(x_mx[1], slice(0, R), x_grp[1][:], E4M3)
+        interleave_on_gpsimd(xm_grp[0][0], xm_raw[0][0])
+        y_banks = (banks[2], banks[3], banks[1], banks[6])
+        turn_y(1, 0, y_banks[0])
+        turn_y(1, 1, y_banks[1])
         weigh(0, 3)
-        turn_h(0, 3, banks[5], nc.scalar.copy)
+        turn_h(0, 3, banks[4], nc.scalar.copy)
+        for c, bank in enumerate((banks[0], banks[1], banks[6], banks[0])):
+            sigmoids(1, c, bank)
+        quantize_xm(0, 0)
         quantize_h(0, 0)
         quantize_h(0, 1)
 
-        spread_wt(1)
         for c in range(2, BLOCKS):
             turn_y(1, c, y_banks[c])
-        for c in range(2):
-            interleave(nc.scalar.copy, xm_grp[0][0], xm_raw[0], c * P, (c + 1) * P)
-        quantize_xm(0, 0)
         for b, k in ((1, 0), (0, 1), (1, 1)):
-            interleave_on_gpsimd(xm_grp[b][k], xm_raw[b][:, :, half(k)])
+            interleave_on_gpsimd(xm_grp[b][k], xm_raw[b][k])
         subtract(1, 0, y_banks[0])
         subtract(1, 1, y_banks[1])
         weigh(1, 0)
-        turn_h(1, 0, banks[4], nc.scalar.copy)
+        turn_h(1, 0, banks[0], nc.vector.tensor_copy)
         subtract(1, 2, y_banks[2])
         weigh(1, 1)
-        turn_h(1, 1, banks[5], nc.scalar.copy)
+        quantize_xm(1, 0)
+        turn_h(1, 1, banks[2], nc.vector.tensor_copy)
         subtract(1, 3, y_banks[3])
         weigh(1, 2)
-        turn_h(1, 2, banks[0], nc.vector.tensor_copy)
-        weigh(1, 3)
-        turn_h(1, 3, banks[2], nc.vector.tensor_copy)
-        quantize_h(1, 0)
-        quantize_h(1, 1)
-        quantize_xm(1, 0)
-
-        product(0, 1, banks[2], nc.vector.tensor_copy)
         quantize_xm(0, 1)
+        turn_h(1, 2, banks[3], nc.vector.tensor_copy)
+        weigh(1, 3)
+        turn_h(1, 3, banks[1], nc.vector.tensor_copy)
+        quantize_h(1, 0)
         quantize_xm(1, 1)
+        quantize_h(1, 1)
+
+        def on_scalar(b, k):
+            product(b, k, banks[{(0, 0): 7, (0, 1): 4, (1, 0): 7, (0, 2): 1, (1, 2): 4}[b, k]], nc.scalar.copy)
+            scatter_on_scalar(b, k)
+
+        on_scalar(0, 0)
+        on_scalar(0, 1)
+        product(0, 3, banks[6], nc.vector.tensor_copy)
         zero(windows[2])
-        for first in (0, 2):
-            for b in range(B):
-                product(b, first, banks[5], nc.scalar.copy)
-                scatter_on_scalar(b, first)
-                if (first, b) != (0, 0):
-                    product(b, first + 1, banks[2], nc.vector.tensor_copy)
-                scatter_on_vector(b, first + 1)
-            store(first)
-            store(first + 1)
+        on_scalar(1, 0)
+        store(0)
+        scatter_on_vector(0, 3)
+        product(1, 3, banks[0], nc.vector.tensor_copy)
+        product(1, 1, banks[2], nc.vector.tensor_copy)
+        scatter_on_vector(1, 3)
+        store(3)
+        scatter_on_vector(1, 1)
+        store(1)
+        on_scalar(0, 2)
+        on_scalar(1, 2)
+        store(2)

@@ -165,14 +165,22 @@ def tile_attend_gnce_w_ts_kernel(tc, xT, w_words, w_scales, y, wt, ts, xm, offs,
 
         def spread_wt(b):
             for j in range(PACK):
-                nc.tensor.transpose(wt_banks[b][:, block(j)], wt_rows[:, b, j : j + 1].to_broadcast([P, P]), ident[:])
+                first = (j // 2) * 2 * P + j % 2
+                nc.tensor.transpose(
+                    wt_banks[b][:, first : first + 2 * P - 1 : 2], wt_rows[:, b, j : j + 1].to_broadcast([P, P]), ident[:]
+                )
 
         def sigmoids(b, c, bank):
             nc.tensor.matmul_mx(
                 out=bank[:], lhsT=w_mx[b][0][:, block(c)].bitcast(E4M3), lhsT_scale=w_mx[b][1][:, block(c)],
                 rhs=x_mx[b][0][:].bitcast(E4M3), rhs_scale=x_mx[b][1][:], start=True, stop=True,
             )
-            nc.scalar.activation(out=sig[b][c][:], in_=bank[:], func=ACT.Sigmoid, scale=ts_inner[b][:, c : c + 1])
+            nc.scalar.activation(
+                out=sig[b][c][:].rearrange("i (u p e) -> i u p e", u=2, e=2),
+                in_=bank[:].rearrange("i (p u e) -> i u p e", u=2, e=2),
+                func=ACT.Sigmoid,
+                scale=ts_inner[b][:, c : c + 1],
+            )
 
         def turn_y(b, c, bank):
             for j in range(PACK):
@@ -180,25 +188,25 @@ def tile_attend_gnce_w_ts_kernel(tc, xT, w_words, w_scales, y, wt, ts, xm, offs,
 
         def subtract(b, c, bank):
             nc.vector.tensor_tensor(
-                out=mid[b][c][:].rearrange("i (p j) -> i p j", j=PACK),
-                in0=sig[b][c][:].rearrange("i (p j) -> i p j", j=PACK),
-                in1=bank[:].rearrange("i (j p) -> i p j", j=PACK),
+                out=mid[b][c][:].rearrange("i (u p e) -> i u p e", u=2, e=2),
+                in0=sig[b][c][:].rearrange("i (u p e) -> i u p e", u=2, e=2),
+                in1=bank[:].rearrange("i (u e p) -> i u p e", u=2, e=2),
                 op=ALU.subtract,
             )
 
         def weigh(b, c):
             nc.vector.scalar_tensor_tensor(
-                out=h_words[b][c][:].bitcast(BF16).rearrange("i (p j) -> i p j", j=PACK),
-                in0=mid[b][c][:].rearrange("i (p j) -> i p j", j=PACK),
+                out=h_words[b][c][:].bitcast(BF16),
+                in0=mid[b][c][:],
                 scalar=ts_outer[b][:, c : c + 1],
-                in1=wt_banks[b][:].rearrange("i (j p) -> i p j", j=PACK),
+                in1=wt_banks[b][:],
                 op0=ALU.mult,
                 op1=ALU.mult,
             )
 
         def turn_h(b, c, bank, engine_copy):
             for u in range(2):
-                nc.tensor.transpose(bank[:, block(u)], h_words[b][c][:, u : 2 * P : 2], ident[:])
+                nc.tensor.transpose(bank[:, block(u)], h_words[b][c][:, block(u)], ident[:])
             engine_copy(
                 out=h_grp[b][:, block(c), :].bitcast(F32), in_=bank[:, 0 : 2 * P].rearrange("p (u i) -> p i u", u=2)
             )

@@ -53,12 +53,19 @@ def tile_attend_gnce_w_ts_kernel(tc, xT, w_words, w_scales, y, wt, ts, xm, offs,
         scale_table = sbuf("scale_table", [P, T], U8)
         nc.gpsimd.memset(scale_table[:].bitcast(I32), 0)
         ts_table = sbuf("ts_table", [P, T], F32)
-        nc.vector.memset(ts_table[:], 0.0)
+        for cols in (slice(0, T // 2 - 1), slice(T // 2 - 1, T)):
+            nc.vector.memset(ts_table[:, cols], 0.0)
         ident = sbuf("ident", [P, P], F32)
         make_identity(nc, ident[:])
 
+        def load_rows(name, rows, at=None):
+            tile = sbuf(name, [P, PACK, rows.shape[1]], F32, at)
+            nc.sync.dma_start(out=tile[:], in_=rows.rearrange("(p j) w -> p j w", j=PACK))
+            return tile
+
         wt_rows = sbuf("wt_rows", [P, B, PACK], F32)
         nc.sync.dma_start(out=wt_rows[:], in_=wt.rearrange("b (p j) o -> p b (j o)", j=PACK))
+        x0_raw = [load_rows("x0_raw0", xT[0][:, half(0)], 54)]
         for q in range(4):
             nc.sync.dma_start(
                 out=scale_table[32 * q : 32 * q + 4, :].bitcast(I32),
@@ -68,69 +75,73 @@ def tile_attend_gnce_w_ts_kernel(tc, xT, w_words, w_scales, y, wt, ts, xm, offs,
         nc.gpsimd.memset(warm[:, 0:1], 0.0)
         nc.scalar.activation(out=warm[:, 1:2], in_=warm[:, 0:1], func=ACT.Sigmoid)
 
-        def load_rows(name, rows):
-            tile = sbuf(name, [P, PACK, rows.shape[1]], F32)
-            nc.sync.dma_start(out=tile[:], in_=rows.rearrange("(p j) w -> p j w", j=PACK))
-            return tile
-
-        x_raw = [load_rows("x_raw0", xT[0])]
+        x0_raw.append(load_rows("x0_raw1", xT[0][:, half(1)]))
         nc.sync.dma_start(out=ts_table[0:1, :], in_=ts[0:1, :])
-        word_table = sbuf("word_table", [P, T], I32, at=0)
+        word_table = sbuf("word_table", [P, T], I32, at=8)
         nc.sync.dma_start(out=word_table[:], in_=w_words[0].rearrange("p t j -> p (t j)").bitcast(I32))
+        x1_raw = [load_rows("x1_raw0", xT[1][:, half(0)])]
         y_raw = [load_rows("y_raw0", y[0])]
-        x_raw.append(load_rows("x_raw1", xT[1]))
+        x1_raw.append(load_rows("x1_raw1", xT[1][:, half(1)]))
         y_raw.append(load_rows("y_raw1", y[1]))
-        xm0_first = load_rows("xm_raw0_0", xm[0][:, half(0)])
-        xm1_whole = load_rows("xm_raw1", xm[1])
-        xm0_second = load_rows("xm_raw0_1", xm[0][:, half(1)])
-        xm_raw = [[xm0_first[:], xm0_second[:]], [xm1_whole[:, :, half(k)] for k in range(2)]]
+        xm0_raw = [load_rows("xm0_raw0", xm[0][:, half(0)])]
+        xm1_raw = load_rows("xm1_raw", xm[1])
+        xm0_raw.append(load_rows("xm0_raw1", xm[0][:, half(1)]))
 
         banks = [psum.tile([P, N], F32, name="bank%d" % k) for k in range(8)]
 
         def mx_tiles(name, width, at=None):
             return sbuf(name + "_codes", [P, width], U32, at), sbuf(name + "_scales", [P, width], U8)
 
-        x_grp = [sbuf("x_grp0", [P, R, PACK], BF16, at=9), sbuf("x_grp1", [P, R, PACK], BF16, at=20)]
-        w_mx = [mx_tiles("w0", N, 8), mx_tiles("w1", N, 10)]
+        x0_grp = sbuf("x0_grp", [P, R, PACK], BF16, at=19)
+        x1_grp = [sbuf("x1_grp%d" % k, [P, HALF, PACK], BF16, at=(12, 32)[k]) for k in range(2)]
+        w_codes = [sbuf("w%d_codes" % b, [P, N], U32, at=(18, 20)[b]) for b in range(B)]
+        w_bytes = sbuf("w_bytes", [P, B * N], U8, at=54)
         windows = [
             sbuf("window0", [P, T], F32),
-            sbuf("window1", [P, T], F32, at=0),
-            sbuf("window2", [P, T], F32, at=40),
-            sbuf("window3", [P, T], F32, at=12),
+            sbuf("window1", [P, T], F32, at=0.5),
+            sbuf("window2", [P, T], F32, at=60),
+            sbuf("window3", [P, T], F32, at=22),
         ]
         ts_listed = [sbuf("ts_listed%d" % b, [P, N], F32) for b in range(B)]
-        ts_inner = [sbuf("ts_inner%d" % b, [P, 32], F32, at=(20, 50)[b])[:, 0:BLOCKS] for b in range(B)]
+        ts_inner0 = sbuf("ts_inner0", [P, BLOCKS], F32, at=32)
         ts_outer = [sbuf("ts_outer%d" % b, [P, BLOCKS], F32) for b in range(B)]
-        sig = [[sbuf("sig%d_%d" % (b, c), [P, R], F32) for c in range(BLOCKS)] for b in range(B)]
-        x_mx = [mx_tiles("x0", R), mx_tiles("x1", R, 24)]
-        mid = [[sbuf("mid%d_%d" % (b, c), [P, R], F32, {(0, 2): 24, (1, 1): 32, (1, 2): 28}.get((b, c))) for c in range(BLOCKS)] for b in range(B)]
+        ts_inner = [ts_inner0, ts_outer[1]]
+        sig = [[sbuf("sig%d_%d" % (b, c), [P, R], F32, {(0, 2): 38}.get((b, c))) for c in range(BLOCKS)] for b in range(B)]
+        mid = [
+            [
+                sbuf("mid%d_%d" % (b, c), [P, R], F32, {(0, 1): 34, (0, 2): 32, (0, 3): 36, (1, 3): 48}.get((b, c)))
+                for c in range(BLOCKS)
+            ]
+            for b in range(B)
+        ]
+        x_mx = [mx_tiles("x0", R), mx_tiles("x1", R, 34)]
         h_words = [
-            [sbuf("h_words%d_%d" % (b, c), [P, R // 2], F32, {(0, 3): 20, (1, 2): 34, (1, 3): 36}.get((b, c))) for c in range(BLOCKS)]
+            [sbuf("h_words%d_%d" % (b, c), [P, R // 2], F32, {(1, 3): 52}.get((b, c))) for c in range(BLOCKS)]
             for b in range(B)
         ]
-        h_grp = [sbuf("h_grp0", [P, N, PACK], BF16), sbuf("h_grp1", [P, N, PACK], BF16)]
+        h_grp = [
+            [sbuf("h%d_grp%d" % (b, k), [P, HALF, PACK], BF16, {(0, 1): 43, (1, 1): 60}.get((b, k))) for k in range(2)]
+            for b in range(B)
+        ]
         h_mx = [mx_tiles("h%d" % b, N) for b in range(B)]
-        xm_grp = [
-            [sbuf("xm_grp%d_%d" % (b, k), [P, HALF, PACK], BF16, ((28, None), (None, 40))[b][k]) for k in range(2)]
-            for b in range(B)
+        xm0_grp = [sbuf("xm0_grp%d" % k, [P, HALF, PACK], BF16, at=(38, 44)[k]) for k in range(2)]
+        xm1_grp = sbuf("xm1_grp", [P, D, PACK], BF16, at=40)
+        xm0_mx = [mx_tiles("xm0_%d" % k, HALF, (36, 49)[k]) for k in range(2)]
+        xm1_mx = mx_tiles("xm1", D, 47)
+        xm_blocks = [
+            [[t[:, block(k % 2)] for t in xm0_mx[k // 2]] for k in range(BLOCKS)],
+            [[t[:, block(k)] for t in xm1_mx] for k in range(BLOCKS)],
         ]
-        xm_mx = [
-            [mx_tiles("xm%d_%d" % (b, k), HALF, ((None, 28), (32, 34))[b][k]) for k in range(2)] for b in range(B)
-        ]
-        dw = [
-            [sbuf("dw%d_%d" % (b, k), [P, N], F32, {(0, 0): 48.0625, (0, 1): 50.0625, (0, 3): 36}.get((b, k))) for k in range(BLOCKS)]
-            for b in range(B)
-        ]
+        dw = [[sbuf("dw%d_%d" % (b, k), [P, N], F32, {(0, 3): 52}.get((b, k))) for k in range(BLOCKS)] for b in range(B)]
         wt_banks = (banks[7], banks[5])
 
-        def interleave(engine_copy, grouped, raw, c0, c1):
+        def interleave(engine_copy, grouped, raw):
             engine_copy(
-                out=grouped[:, c0:c1, :].rearrange("p (c i) t -> p c t i", i=RUN),
-                in_=raw[:, :, c0:c1].rearrange("p t (c i) -> p c t i", i=RUN),
+                out=grouped.rearrange("p (c i) t -> p c t i", i=RUN), in_=raw.rearrange("p t (c i) -> p c t i", i=RUN)
             )
 
         def interleave_on_gpsimd(grouped, raw):
-            for first in range(0, HALF, CAST_COLS):
+            for first in range(0, raw.shape[2], CAST_COLS):
                 nc.gpsimd.tensor_scalar(
                     out=grouped[:, first : first + CAST_COLS, :],
                     in0=raw[:, :, first : first + CAST_COLS].rearrange("p t w -> p w t"),
@@ -146,12 +157,13 @@ def tile_attend_gnce_w_ts_kernel(tc, xT, w_words, w_scales, y, wt, ts, xm, offs,
             for c0 in range(0, T, ZERO_COLS):
                 nc.gpsimd.memset(window[:, c0 : c0 + ZERO_COLS], 0.0)
 
-        def gather_scales(b):
-            nc.vector.tensor_copy(out=w_mx[b][1][:], in_=scale_table[:].indirect(listed(b, 0, N)))
+        def gather_scales():
+            nc.vector.tensor_copy(out=w_bytes[:], in_=scale_table[:].indirect(offsets[:]))
 
         def gather_words(b, first, count):
             nc.vector.tensor_copy(
-                out=w_mx[b][0][:, first : first + count], in_=word_table[:].bitcast(U32).indirect(listed(b, first, count))
+                out=w_codes[b][:, first : first + count],
+                in_=word_table[:].bitcast(U32).indirect(listed(b, first, count)),
             )
 
         def gather_ts(b):
@@ -160,8 +172,9 @@ def tile_attend_gnce_w_ts_kernel(tc, xT, w_words, w_scales, y, wt, ts, xm, offs,
         def turn_ts(b, bank):
             for c in range(BLOCKS):
                 nc.tensor.transpose(bank[:, block(c)], ts_listed[b][:, block(c)], ident[:])
-            nc.scalar.copy(out=ts_inner[b], in_=bank[:, 0:N:P])
-            nc.scalar.copy(out=ts_outer[b][:], in_=bank[:, 0:N:P])
+
+        def keep_ts(columns, bank):
+            nc.scalar.copy(out=columns[:], in_=bank[:, 0:N:P])
 
         def spread_wt(b):
             for j in range(PACK):
@@ -170,11 +183,13 @@ def tile_attend_gnce_w_ts_kernel(tc, xT, w_words, w_scales, y, wt, ts, xm, offs,
                     wt_banks[b][:, first : first + 2 * P - 1 : 2], wt_rows[:, b, j : j + 1].to_broadcast([P, P]), ident[:]
                 )
 
-        def sigmoids(b, c, bank):
+        def scores(b, c, bank):
             nc.tensor.matmul_mx(
-                out=bank[:], lhsT=w_mx[b][0][:, block(c)].bitcast(E4M3), lhsT_scale=w_mx[b][1][:, block(c)],
+                out=bank[:], lhsT=w_codes[b][:, block(c)].bitcast(E4M3), lhsT_scale=w_bytes[:, block(b * BLOCKS + c)],
                 rhs=x_mx[b][0][:].bitcast(E4M3), rhs_scale=x_mx[b][1][:], start=True, stop=True,
             )
+
+        def sigmoid(b, c, bank):
             nc.scalar.activation(
                 out=sig[b][c][:].rearrange("i (u p e) -> i u p e", u=2, e=2),
                 in_=bank[:].rearrange("i (p u e) -> i u p e", u=2, e=2),
@@ -204,124 +219,149 @@ def tile_attend_gnce_w_ts_kernel(tc, xT, w_words, w_scales, y, wt, ts, xm, offs,
                 op1=ALU.mult,
             )
 
-        def turn_h(b, c, bank, engine_copy):
+        def turn_h(b, c, bank):
             for u in range(2):
                 nc.tensor.transpose(bank[:, block(u)], h_words[b][c][:, block(u)], ident[:])
+
+        def group_h(b, c, bank, engine_copy):
             engine_copy(
-                out=h_grp[b][:, block(c), :].bitcast(F32), in_=bank[:, 0 : 2 * P].rearrange("p (u i) -> p i u", u=2)
+                out=h_grp[b][c // 2][:, block(c % 2), :].bitcast(F32), in_=bank[:, 0 : 2 * P].rearrange("p (u i) -> p i u", u=2)
             )
 
         def quantize_h(b, k):
-            quantize(h_mx[b], half(k), h_grp[b][:, half(k), :], E5M2)
+            quantize(h_mx[b], half(k), h_grp[b][k][:], E5M2)
 
-        def quantize_xm(b, k):
-            quantize(xm_mx[b][k], slice(0, HALF), xm_grp[b][k][:], E4M3)
-
-        def product(b, k, bank, engine_copy):
-            codes, scales = xm_mx[b][k // 2]
+        def product(b, k, bank, slots=slice(0, N)):
+            codes, scales = xm_blocks[b][k]
             nc.tensor.matmul_mx(
-                out=bank[:], lhsT=codes[:, block(k % 2)].bitcast(E4M3), lhsT_scale=scales[:, block(k % 2)],
-                rhs=h_mx[b][0][:].bitcast(E5M2), rhs_scale=h_mx[b][1][:], start=True, stop=True,
+                out=bank[:, slots], lhsT=codes.bitcast(E4M3), lhsT_scale=scales,
+                rhs=h_mx[b][0][:, slots].bitcast(E5M2), rhs_scale=h_mx[b][1][:, slots], start=True, stop=True,
             )
-            engine_copy(out=dw[b][k][:], in_=bank[:])
+
+        def empty(b, k, bank, engine_copy, slots=slice(0, N)):
+            engine_copy(out=dw[b][k][:, slots], in_=bank[:, slots])
 
         def scatter_on_vector(b, k):
             nc.vector.tensor_copy(out=windows[k][:].indirect(listed(b, 0, N)), in_=dw[b][k][:])
 
-        def scatter_on_scalar(b, k):
-            for first in (0, HALF):
-                nc.scalar.activation(
-                    out=windows[k][:].indirect(listed(b, first, HALF)), in_=dw[b][k][:, first : first + HALF], func=ACT.Copy
-                )
+        def scatter_half(b, k, part, values):
+            nc.scalar.activation(out=windows[k][:].indirect(listed(b, part * HALF, HALF)), in_=values, func=ACT.Copy)
 
-        def store(k):
-            (nc.scalar if k % 2 == 0 else nc.sync).dma_start(out=out[block(k), :], in_=windows[k][:])
+        def scatter_on_scalar(b, k):
+            for part in range(2):
+                scatter_half(b, k, part, dw[b][k][:, half(part)])
+
+        def store(k, queue):
+            queue.dma_start(out=out[block(k), :], in_=windows[k][:])
+
+        scalar_copy, vector_copy = nc.scalar.copy, nc.vector.tensor_copy
 
         zero(windows[0])
-        gather_scales(0)
-        gather_scales(1)
+        interleave(vector_copy, x0_grp[:, half(0), :], x0_raw[0][:])
+        gather_scales()
+        interleave_on_gpsimd(x0_grp[:, half(1), :], x0_raw[1])
         gather_ts(0)
         turn_ts(0, banks[4])
+        keep_ts(ts_inner0, banks[4])
+        keep_ts(ts_outer[0], banks[4])
         gather_ts(1)
         spread_wt(0)
         spread_wt(1)
-        interleave(nc.vector.tensor_copy, x_grp[0], x_raw[0], 0, R)
-        quantize(x_mx[0], slice(0, R), x_grp[0][:], E4M3)
+        quantize(x_mx[0], slice(0, R), x0_grp[:], E4M3)
         for k in range(2):
             gather_words(0, k * HALF, HALF)
         gather_words(1, 0, N)
         zero(windows[3])
         zero(windows[1])
+        interleave(vector_copy, x1_grp[0][:], x1_raw[0][:])
 
         for c in range(BLOCKS):
-            sigmoids(0, c, banks[c])
+            scores(0, c, banks[c])
+            sigmoid(0, c, banks[c])
         for c in range(BLOCKS):
             turn_y(0, c, banks[c])
-        for k in range(2):
-            interleave(nc.scalar.copy, x_grp[1], x_raw[1], k * HALF, (k + 1) * HALF)
+        interleave(scalar_copy, x1_grp[1][:], x1_raw[1][:])
         subtract(0, 0, banks[0])
         turn_ts(1, banks[0])
+        keep_ts(ts_outer[1], banks[0])
         subtract(0, 1, banks[1])
         weigh(0, 0)
-        turn_h(0, 0, banks[4], nc.scalar.copy)
-        subtract(0, 2, banks[2])
+        turn_h(0, 0, banks[4])
+        group_h(0, 0, banks[4], scalar_copy)
         weigh(0, 1)
-        turn_h(0, 1, banks[4], nc.scalar.copy)
+        turn_h(0, 1, banks[6])
+        group_h(0, 1, banks[6], scalar_copy)
+        for k in range(2):
+            quantize(x_mx[1], half(k), x1_grp[k][:], E4M3)
+        for c, bank in enumerate((banks[0], banks[1], banks[4], banks[6])):
+            scores(1, c, bank)
+            sigmoid(1, c, bank)
+        subtract(0, 2, banks[2])
+        interleave_on_gpsimd(xm0_grp[0], xm0_raw[0])
         subtract(0, 3, banks[3])
         weigh(0, 2)
-        turn_h(0, 2, banks[4], nc.scalar.copy)
-        quantize(x_mx[1], slice(0, R), x_grp[1][:], E4M3)
-        interleave_on_gpsimd(xm_grp[0][0], xm_raw[0][0])
-        y_banks = (banks[2], banks[3], banks[1], banks[6])
-        turn_y(1, 0, y_banks[0])
-        turn_y(1, 1, y_banks[1])
+        turn_h(0, 2, banks[2])
         weigh(0, 3)
-        turn_h(0, 3, banks[4], nc.scalar.copy)
-        for c, bank in enumerate((banks[0], banks[1], banks[6], banks[0])):
-            sigmoids(1, c, bank)
-        quantize_xm(0, 0)
+        turn_h(0, 3, banks[3])
         quantize_h(0, 0)
+        quantize(xm0_mx[0], slice(0, HALF), xm0_grp[0][:], E4M3)
+        product(0, 0, banks[7], half(0))
+        empty(0, 0, banks[7], scalar_copy, half(0))
+        scatter_half(0, 0, 0, dw[0][0][:, half(0)])
+        y_banks = (banks[4], banks[2], banks[3], banks[4])
+        turn_y(1, 0, y_banks[0])
+        group_h(0, 2, banks[2], vector_copy)
+        turn_y(1, 1, y_banks[1])
+        group_h(0, 3, banks[3], vector_copy)
         quantize_h(0, 1)
+        interleave_on_gpsimd(xm1_grp, xm1_raw)
+        interleave_on_gpsimd(xm0_grp[1], xm0_raw[1])
+        product(0, 0, banks[0], half(1))
+        turn_y(1, 2, y_banks[2])
 
-        for c in range(2, BLOCKS):
-            turn_y(1, c, y_banks[c])
-        for b, k in ((1, 0), (0, 1), (1, 1)):
-            interleave_on_gpsimd(xm_grp[b][k], xm_raw[b][k])
         subtract(1, 0, y_banks[0])
+        turn_y(1, 3, y_banks[3])
+        product(0, 1, banks[1])
         subtract(1, 1, y_banks[1])
         weigh(1, 0)
-        turn_h(1, 0, banks[0], nc.vector.tensor_copy)
-        subtract(1, 2, y_banks[2])
+        turn_h(1, 0, banks[6])
         weigh(1, 1)
-        quantize_xm(1, 0)
-        turn_h(1, 1, banks[2], nc.vector.tensor_copy)
+        turn_h(1, 1, banks[2])
+        subtract(1, 2, y_banks[2])
+        group_h(1, 0, banks[6], vector_copy)
         subtract(1, 3, y_banks[3])
+        group_h(1, 1, banks[2], vector_copy)
         weigh(1, 2)
-        quantize_xm(0, 1)
-        turn_h(1, 2, banks[3], nc.vector.tensor_copy)
+        turn_h(1, 2, banks[3])
         weigh(1, 3)
-        turn_h(1, 3, banks[1], nc.vector.tensor_copy)
+        turn_h(1, 3, banks[4])
         quantize_h(1, 0)
-        quantize_xm(1, 1)
+        quantize(xm0_mx[1], slice(0, HALF), xm0_grp[1][:], E4M3)
+        product(0, 3, banks[7])
+        quantize(xm1_mx, slice(0, D), xm1_grp[:], E4M3)
+        group_h(1, 2, banks[3], vector_copy)
+        group_h(1, 3, banks[4], vector_copy)
         quantize_h(1, 1)
+        zero(windows[2])
 
-        def on_scalar(b, k):
-            product(b, k, banks[{(0, 0): 7, (0, 1): 4, (1, 0): 7, (0, 2): 1, (1, 2): 4}[b, k]], nc.scalar.copy)
+        def on_scalar(b, k, bank):
+            product(b, k, bank)
+            empty(b, k, bank, scalar_copy)
             scatter_on_scalar(b, k)
 
-        on_scalar(0, 0)
-        on_scalar(0, 1)
-        product(0, 3, banks[6], nc.vector.tensor_copy)
-        zero(windows[2])
-        on_scalar(1, 0)
-        store(0)
+        empty(0, 0, banks[0], scalar_copy, half(1))
+        scatter_half(0, 0, 1, dw[0][0][:, half(1)])
+        empty(0, 1, banks[1], scalar_copy)
+        scatter_on_scalar(0, 1)
+        on_scalar(1, 0, banks[0])
+        store(0, nc.scalar)
+        empty(0, 3, banks[7], vector_copy)
         scatter_on_vector(0, 3)
-        product(1, 3, banks[0], nc.vector.tensor_copy)
-        product(1, 1, banks[2], nc.vector.tensor_copy)
-        scatter_on_vector(1, 3)
-        store(3)
-        scatter_on_vector(1, 1)
-        store(1)
-        on_scalar(0, 2)
-        on_scalar(1, 2)
-        store(2)
+        for k, bank in ((3, banks[6]), (1, banks[2])):
+            product(1, k, bank)
+            empty(1, k, bank, vector_copy)
+            scatter_on_vector(1, k)
+            store(k, nc.sync)
+        on_scalar(0, 2, banks[1])
+        on_scalar(1, 2, banks[5])
+        store(2, nc.scalar)

@@ -22,7 +22,7 @@ PACK = 4
 BLOCKS = 4
 HALF = N // 2
 RUN = 4
-ZERO_COLS = 1024
+ZERO_COLS = 512
 CAST_COLS = 128
 
 
@@ -65,7 +65,6 @@ def tile_attend_gnce_w_ts_kernel(tc, xT, w_words, w_scales, y, wt, ts, xm, offs,
 
         wt_rows = sbuf("wt_rows", [P, B, PACK], F32)
         nc.sync.dma_start(out=wt_rows[:], in_=wt.rearrange("b (p j) o -> p b (j o)", j=PACK))
-        x0_raw = [load_rows("x0_raw0", xT[0][:, half(0)], 54)]
         for q in range(4):
             nc.sync.dma_start(
                 out=scale_table[32 * q : 32 * q + 4, :].bitcast(I32),
@@ -75,17 +74,17 @@ def tile_attend_gnce_w_ts_kernel(tc, xT, w_words, w_scales, y, wt, ts, xm, offs,
         nc.gpsimd.memset(warm[:, 0:1], 0.0)
         nc.scalar.activation(out=warm[:, 1:2], in_=warm[:, 0:1], func=ACT.Sigmoid)
 
-        x0_raw.append(load_rows("x0_raw1", xT[0][:, half(1)]))
+        x0_raw = load_rows("x0_raw", xT[0])
         nc.sync.dma_start(out=ts_table[0:1, :], in_=ts[0:1, :])
-        word_table = sbuf("word_table", [P, T], I32, at=8)
+        word_table = sbuf("word_table", [P, T], I32, at=9)
         nc.sync.dma_start(out=word_table[:], in_=w_words[0].rearrange("p t j -> p (t j)").bitcast(I32))
-        x1_raw = [load_rows("x1_raw0", xT[1][:, half(0)])]
+        x1_raw = [load_rows("x1_raw0", xT[1][:, half(0)], 0)]
         y_raw = [load_rows("y_raw0", y[0])]
         x1_raw.append(load_rows("x1_raw1", xT[1][:, half(1)]))
-        y_raw.append(load_rows("y_raw1", y[1]))
         xm0_raw = [load_rows("xm0_raw0", xm[0][:, half(0)])]
-        xm1_raw = load_rows("xm1_raw", xm[1])
+        y_raw.append(load_rows("y_raw1", y[1]))
         xm0_raw.append(load_rows("xm0_raw1", xm[0][:, half(1)]))
+        xm1_raw = load_rows("xm1_raw", xm[1])
 
         banks = [psum.tile([P, N], F32, name="bank%d" % k) for k in range(8)]
 
@@ -95,7 +94,7 @@ def tile_attend_gnce_w_ts_kernel(tc, xT, w_words, w_scales, y, wt, ts, xm, offs,
         x0_grp = sbuf("x0_grp", [P, R, PACK], BF16, at=19)
         x1_grp = [sbuf("x1_grp%d" % k, [P, HALF, PACK], BF16, at=(12, 32)[k]) for k in range(2)]
         w_codes = [sbuf("w%d_codes" % b, [P, N], U32, at=(18, 20)[b]) for b in range(B)]
-        w_bytes = sbuf("w_bytes", [P, B * N], U8, at=54)
+        w_bytes = sbuf("w_bytes", [P, B * N], U8)
         windows = [
             sbuf("window0", [P, T], F32),
             sbuf("window1", [P, T], F32, at=0.5),
@@ -106,7 +105,7 @@ def tile_attend_gnce_w_ts_kernel(tc, xT, w_words, w_scales, y, wt, ts, xm, offs,
         ts_inner0 = sbuf("ts_inner0", [P, BLOCKS], F32, at=32)
         ts_outer = [sbuf("ts_outer%d" % b, [P, BLOCKS], F32) for b in range(B)]
         ts_inner = [ts_inner0, ts_outer[1]]
-        sig = [[sbuf("sig%d_%d" % (b, c), [P, R], F32, {(0, 2): 38}.get((b, c))) for c in range(BLOCKS)] for b in range(B)]
+        sig = [[sbuf("sig%d_%d" % (b, c), [P, R], F32) for c in range(BLOCKS)] for b in range(B)]
         mid = [
             [
                 sbuf("mid%d_%d" % (b, c), [P, R], F32, {(0, 1): 34, (0, 2): 32, (0, 3): 36, (1, 3): 48}.get((b, c)))
@@ -124,7 +123,7 @@ def tile_attend_gnce_w_ts_kernel(tc, xT, w_words, w_scales, y, wt, ts, xm, offs,
             for b in range(B)
         ]
         h_mx = [mx_tiles("h%d" % b, N) for b in range(B)]
-        xm0_grp = [sbuf("xm0_grp%d" % k, [P, HALF, PACK], BF16, at=(38, 44)[k]) for k in range(2)]
+        xm0_grp = [sbuf("xm0_grp%d" % k, [P, HALF, PACK], BF16, at=(12, 44)[k]) for k in range(2)]
         xm1_grp = sbuf("xm1_grp", [P, D, PACK], BF16, at=40)
         xm0_mx = [mx_tiles("xm0_%d" % k, HALF, (36, 49)[k]) for k in range(2)]
         xm1_mx = mx_tiles("xm1", D, 47)
@@ -257,9 +256,7 @@ def tile_attend_gnce_w_ts_kernel(tc, xT, w_words, w_scales, y, wt, ts, xm, offs,
         scalar_copy, vector_copy = nc.scalar.copy, nc.vector.tensor_copy
 
         zero(windows[0])
-        interleave(vector_copy, x0_grp[:, half(0), :], x0_raw[0][:])
         gather_scales()
-        interleave_on_gpsimd(x0_grp[:, half(1), :], x0_raw[1])
         gather_ts(0)
         turn_ts(0, banks[4])
         keep_ts(ts_inner0, banks[4])
@@ -267,13 +264,14 @@ def tile_attend_gnce_w_ts_kernel(tc, xT, w_words, w_scales, y, wt, ts, xm, offs,
         gather_ts(1)
         spread_wt(0)
         spread_wt(1)
+        interleave(vector_copy, x0_grp[:], x0_raw[:])
         quantize(x_mx[0], slice(0, R), x0_grp[:], E4M3)
         for k in range(2):
             gather_words(0, k * HALF, HALF)
         gather_words(1, 0, N)
         zero(windows[3])
-        zero(windows[1])
         interleave(vector_copy, x1_grp[0][:], x1_raw[0][:])
+        zero(windows[1])
 
         for c in range(BLOCKS):
             scores(0, c, banks[c])
@@ -291,31 +289,31 @@ def tile_attend_gnce_w_ts_kernel(tc, xT, w_words, w_scales, y, wt, ts, xm, offs,
         weigh(0, 1)
         turn_h(0, 1, banks[6])
         group_h(0, 1, banks[6], scalar_copy)
-        for k in range(2):
+        for k in (1, 0):
             quantize(x_mx[1], half(k), x1_grp[k][:], E4M3)
+        interleave_on_gpsimd(xm0_grp[0], xm0_raw[0])
         for c, bank in enumerate((banks[0], banks[1], banks[4], banks[6])):
             scores(1, c, bank)
             sigmoid(1, c, bank)
         subtract(0, 2, banks[2])
-        interleave_on_gpsimd(xm0_grp[0], xm0_raw[0])
         subtract(0, 3, banks[3])
         weigh(0, 2)
         turn_h(0, 2, banks[2])
         weigh(0, 3)
         turn_h(0, 3, banks[3])
         quantize_h(0, 0)
+        group_h(0, 2, banks[2], vector_copy)
         quantize(xm0_mx[0], slice(0, HALF), xm0_grp[0][:], E4M3)
         product(0, 0, banks[7], half(0))
         empty(0, 0, banks[7], scalar_copy, half(0))
         scatter_half(0, 0, 0, dw[0][0][:, half(0)])
         y_banks = (banks[4], banks[2], banks[3], banks[4])
         turn_y(1, 0, y_banks[0])
-        group_h(0, 2, banks[2], vector_copy)
         turn_y(1, 1, y_banks[1])
         group_h(0, 3, banks[3], vector_copy)
         quantize_h(0, 1)
-        interleave_on_gpsimd(xm1_grp, xm1_raw)
         interleave_on_gpsimd(xm0_grp[1], xm0_raw[1])
+        interleave_on_gpsimd(xm1_grp, xm1_raw)
         product(0, 0, banks[0], half(1))
         turn_y(1, 2, y_banks[2])
 

@@ -21,6 +21,7 @@ P = 128
 PACK = 4
 BLOCKS = 4
 HALF = N // 2
+LONG = 384
 RUN = 4
 ZERO_COLS = 512
 CAST_COLS = 128
@@ -131,7 +132,10 @@ def tile_attend_gnce_w_ts_kernel(tc, xT, w_words, w_scales, y, wt, ts, xm, offs,
             [[t[:, block(k % 2)] for t in xm0_mx[k // 2]] for k in range(BLOCKS)],
             [[t[:, block(k)] for t in xm1_mx] for k in range(BLOCKS)],
         ]
-        dw = [[sbuf("dw%d_%d" % (b, k), [P, N], F32, {(0, 3): 52}.get((b, k))) for k in range(BLOCKS)] for b in range(B)]
+        dw = [[sbuf("dw%d_%d" % (b, k), [P, N], F32, {(0, 3): 52}.get((b, k))) if k != 2 else None for k in range(BLOCKS)] for b in range(B)]
+        dw_both = sbuf("dw_both", [P, B * N], F32)
+        for b in range(B):
+            dw[b][2] = dw_both[:, b * N : (b + 1) * N]
         wt_banks = (banks[7], banks[5])
 
         def interleave(engine_copy, grouped, raw):
@@ -245,6 +249,11 @@ def tile_attend_gnce_w_ts_kernel(tc, xT, w_words, w_scales, y, wt, ts, xm, offs,
 
         def scatter_half(b, k, part, values):
             nc.scalar.activation(out=windows[k][:].indirect(listed(b, part * HALF, HALF)), in_=values, func=ACT.Copy)
+
+        def scatter_both(first, count):
+            nc.scalar.activation(
+                out=windows[2][:].indirect(listed(0, first, count)), in_=dw_both[:, first : first + count], func=ACT.Copy
+            )
 
         def scatter_on_scalar(b, k):
             for part in range(2):
@@ -360,6 +369,9 @@ def tile_attend_gnce_w_ts_kernel(tc, xT, w_words, w_scales, y, wt, ts, xm, offs,
             empty(1, k, bank, vector_copy)
             scatter_on_vector(1, k)
             store(k, nc.sync)
-        on_scalar(0, 2, banks[1])
-        on_scalar(1, 2, banks[5])
+        for b, bank in enumerate((banks[1], banks[5])):
+            product(b, 2, bank)
+            empty(b, 2, bank, scalar_copy)
+        for first in range(0, B * N, LONG):
+            scatter_both(first, min(LONG, B * N - first))
         store(2, nc.scalar)

from contextlib import ExitStack

import concourse.mybir as mybir
from concourse.masks import make_identity

B, N, T, D, R = 2, 512, 2048, 512, 512
FLOPS = 2 * 2 * B * N * D * R

F32 = mybir.dt.float32
BF16 = mybir.dt.bfloat16
I32 = mybir.dt.int32
U32 = mybir.dt.uint32
U16 = mybir.dt.uint16
U8 = mybir.dt.uint8
E4M3 = mybir.dt.float8_e4m3fn_x4
E5M2 = mybir.dt.float8_e5m2_x4
ALU = mybir.AluOpType
ACT = mybir.ActivationFunctionType

P = 128
PACK = 4
BLOCKS = 4
HALF = N // 2
LONG = 384
RUN = 4
ZERO_COLS = 512
CAST_COLS = 128


def tile_attend_gnce_w_ts_kernel(tc, xT, w_words, w_scales, y, wt, ts, xm, offs, out):
    nc = tc.nc
    with ExitStack() as ctx:
        keep = ctx.enter_context(tc.tile_pool(name="keep", bufs=1))
        shared = ctx.enter_context(tc.tile_pool(name="shared", bufs=1))
        psum = ctx.enter_context(tc.psum_pool(name="psum", bufs=1))

        def sbuf(name, shape, dtype, at=None):
            if at is None:
                return keep.tile(shape, dtype, name=name, align_bytes=64)
            return shared.tile(shape, dtype, name=name, align_bytes=64, offset=int(at * 1024))

        def block(c):
            return slice(c * P, (c + 1) * P)

        def half(k):
            return slice(k * HALF, (k + 1) * HALF)

        offsets = keep.tile([P, B * N // 16], U16, name="offsets")
        nc.sync.dma_start(offsets[:], offs)

        def listed(b, first, count):
            return offsets[:, (b * N + first) // 16 : (b * N + first + count) // 16]

        scale_table = sbuf("scale_table", [P, T], U8)
        nc.gpsimd.memset(scale_table[:].bitcast(I32), 0)
        ts_table = sbuf("ts_table", [P, T], F32)
        for cols in (slice(0, T // 2 - 1), slice(T // 2 - 1, T)):
            nc.vector.memset(ts_table[:, cols], 0.0)
        ident = sbuf("ident", [P, P], F32)
        make_identity(nc, ident[:])

        def load_rows(name, rows, at=None):
            tile = sbuf(name, [P, PACK, rows.shape[1]], F32, at)
            nc.sync.dma_start(out=tile[:], in_=rows.rearrange("(p j) w -> p j w", j=PACK))
            return tile

        wt_rows = sbuf("wt_rows", [P, B, PACK], F32)
        nc.sync.dma_start(out=wt_rows[:], in_=wt.rearrange("b (p j) o -> p b (j o)", j=PACK))
        for q in range(4):
            nc.sync.dma_start(
                out=scale_table[32 * q : 32 * q + 4, :].bitcast(I32),
                in_=w_scales[0, 4 * q : 4 * q + 4, :].bitcast(I32),
            )
        warm = sbuf("warm", [P, 2], F32)
        nc.gpsimd.memset(warm[:, 0:1], 0.0)
        nc.scalar.activation(out=warm[:, 1:2], in_=warm[:, 0:1], func=ACT.Sigmoid)

        x0_raw = load_rows("x0_raw", xT[0])
        nc.sync.dma_start(out=ts_table[0:1, :], in_=ts[0:1, :])
        word_table = sbuf("word_table", [P, T], I32, at=9)
        nc.sync.dma_start(out=word_table[:], in_=w_words[0].rearrange("p t j -> p (t j)").bitcast(I32))
        x1_raw = [load_rows("x1_raw0", xT[1][:, half(0)], 0)]
        y_raw = [load_rows("y_raw0", y[0])]
        x1_raw.append(load_rows("x1_raw1", xT[1][:, half(1)]))
        xm0_raw = [load_rows("xm0_raw0", xm[0][:, half(0)])]
        y_raw.append(load_rows("y_raw1", y[1]))
        xm0_raw.append(load_rows("xm0_raw1", xm[0][:, half(1)]))
        xm1_raw = load_rows("xm1_raw", xm[1])

        banks = [psum.tile([P, N], F32, name="bank%d" % k) for k in range(8)]

        def mx_tiles(name, width, at=None):
            return sbuf(name + "_codes", [P, width], U32, at), sbuf(name + "_scales", [P, width], U8)

        x0_grp = sbuf("x0_grp", [P, R, PACK], BF16, at=19)
        x1_grp = [sbuf("x1_grp%d" % k, [P, HALF, PACK], BF16, at=(12, 32)[k]) for k in range(2)]
        w_codes = [sbuf("w%d_codes" % b, [P, N], U32, at=(18, 20)[b]) for b in range(B)]
        w_bytes = sbuf("w_bytes", [P, B * N], U8)
        windows = [
            sbuf("window0", [P, T], F32),
            sbuf("window1", [P, T], F32, at=0.5),
            sbuf("window2", [P, T], F32, at=60),
            sbuf("window3", [P, T], F32, at=22),
        ]
        ts_listed = [sbuf("ts_listed%d" % b, [P, N], F32) for b in range(B)]
        ts_inner0 = sbuf("ts_inner0", [P, BLOCKS], F32, at=32)
        ts_outer = [sbuf("ts_outer%d" % b, [P, BLOCKS], F32) for b in range(B)]
        ts_inner = [ts_inner0, ts_outer[1]]
        sig = [[sbuf("sig%d_%d" % (b, c), [P, R], F32) for c in range(BLOCKS)] for b in range(B)]
        mid = [
            [
                sbuf("mid%d_%d" % (b, c), [P, R], F32, {(0, 1): 34, (0, 2): 32, (0, 3): 36, (1, 3): 48}.get((b, c)))
                for c in range(BLOCKS)
            ]
            for b in range(B)
        ]
        x_mx = [mx_tiles("x0", R), mx_tiles("x1", R, 34)]
        h_words = [
            [sbuf("h_words%d_%d" % (b, c), [P, R // 2], F32, {(1, 3): 52}.get((b, c))) for c in range(BLOCKS)]
            for b in range(B)
        ]
        h_grp = [
            [sbuf("h%d_grp%d" % (b, k), [P, HALF, PACK], BF16, {(0, 1): 43, (1, 1): 60}.get((b, k))) for k in range(2)]
            for b in range(B)
        ]
        h_mx = [mx_tiles("h%d" % b, N) for b in range(B)]
        xm0_grp = [sbuf("xm0_grp%d" % k, [P, HALF, PACK], BF16, at=(12, 44)[k]) for k in range(2)]
        xm1_grp = sbuf("xm1_grp", [P, D, PACK], BF16, at=40)
        xm0_mx = [mx_tiles("xm0_%d" % k, HALF, (36, 49)[k]) for k in range(2)]
        xm1_mx = mx_tiles("xm1", D, 47)
        xm_blocks = [
            [[t[:, block(k % 2)] for t in xm0_mx[k // 2]] for k in range(BLOCKS)],
            [[t[:, block(k)] for t in xm1_mx] for k in range(BLOCKS)],
        ]
        dw = [[sbuf("dw%d_%d" % (b, k), [P, N], F32, {(0, 3): 52}.get((b, k))) if k != 2 else None for k in range(BLOCKS)] for b in range(B)]
        dw_both = sbuf("dw_both", [P, B * N], F32)
        for b in range(B):
            dw[b][2] = dw_both[:, b * N : (b + 1) * N]
        wt_banks = (banks[7], banks[5])

        def interleave(engine_copy, grouped, raw):
            engine_copy(
                out=grouped.rearrange("p (c i) t -> p c t i", i=RUN), in_=raw.rearrange("p t (c i) -> p c t i", i=RUN)
            )

        def interleave_on_gpsimd(grouped, raw):
            for first in range(0, raw.shape[2], CAST_COLS):
                nc.gpsimd.tensor_scalar(
                    out=grouped[:, first : first + CAST_COLS, :],
                    in0=raw[:, :, first : first + CAST_COLS].rearrange("p t w -> p w t"),
                    scalar1=1.0, scalar2=0.0, op0=ALU.mult, op1=ALU.add,
                )

        def quantize(pair, cols, grouped, fmt):
            nc.vector.quantize_mx(
                out=pair[0][:, cols].bitcast(fmt), scales=pair[1][:, cols], in_=grouped.rearrange("p w t -> p (w t)")
            )

        def zero(window):
            for c0 in range(0, T, ZERO_COLS):
                nc.gpsimd.memset(window[:, c0 : c0 + ZERO_COLS], 0.0)

        def gather_scales():
            nc.vector.tensor_copy(out=w_bytes[:], in_=scale_table[:].indirect(offsets[:]))

        def gather_words(b, first, count):
            nc.vector.tensor_copy(
                out=w_codes[b][:, first : first + count],
                in_=word_table[:].bitcast(U32).indirect(listed(b, first, count)),
            )

        def gather_ts(b):
            nc.scalar.activation(out=ts_listed[b][:], in_=ts_table[:].indirect(listed(b, 0, N)), func=ACT.Copy)

        def turn_ts(b, bank):
            for c in range(BLOCKS):
                nc.tensor.transpose(bank[:, block(c)], ts_listed[b][:, block(c)], ident[:])

        def keep_ts(columns, bank):
            nc.scalar.copy(out=columns[:], in_=bank[:, 0:N:P])

        def spread_wt(b):
            for j in range(PACK):
                first = (j // 2) * 2 * P + j % 2
                nc.tensor.transpose(
                    wt_banks[b][:, first : first + 2 * P - 1 : 2], wt_rows[:, b, j : j + 1].to_broadcast([P, P]), ident[:]
                )

        def scores(b, c, bank):
            nc.tensor.matmul_mx(
                out=bank[:], lhsT=w_codes[b][:, block(c)].bitcast(E4M3), lhsT_scale=w_bytes[:, block(b * BLOCKS + c)],
                rhs=x_mx[b][0][:].bitcast(E4M3), rhs_scale=x_mx[b][1][:], start=True, stop=True,
            )

        def sigmoid(b, c, bank):
            nc.scalar.activation(
                out=sig[b][c][:].rearrange("i (u p e) -> i u p e", u=2, e=2),
                in_=bank[:].rearrange("i (p u e) -> i u p e", u=2, e=2),
                func=ACT.Sigmoid,
                scale=ts_inner[b][:, c : c + 1],
            )

        def turn_y(b, c, bank):
            for j in range(PACK):
                nc.tensor.transpose(bank[:, block(j)], y_raw[b][:, j, block(c)], ident[:])

        def subtract(b, c, bank):
            nc.vector.tensor_tensor(
                out=mid[b][c][:].rearrange("i (u p e) -> i u p e", u=2, e=2),
                in0=sig[b][c][:].rearrange("i (u p e) -> i u p e", u=2, e=2),
                in1=bank[:].rearrange("i (u e p) -> i u p e", u=2, e=2),
                op=ALU.subtract,
            )

        def weigh(b, c):
            nc.vector.scalar_tensor_tensor(
                out=h_words[b][c][:].bitcast(BF16),
                in0=mid[b][c][:],
                scalar=ts_outer[b][:, c : c + 1],
                in1=wt_banks[b][:],
                op0=ALU.mult,
                op1=ALU.mult,
            )

        def turn_h(b, c, bank):
            for u in range(2):
                nc.tensor.transpose(bank[:, block(u)], h_words[b][c][:, block(u)], ident[:])

        def group_h(b, c, bank, engine_copy):
            engine_copy(
                out=h_grp[b][c // 2][:, block(c % 2), :].bitcast(F32), in_=bank[:, 0 : 2 * P].rearrange("p (u i) -> p i u", u=2)
            )

        def quantize_h(b, k):
            quantize(h_mx[b], half(k), h_grp[b][k][:], E5M2)

        def product(b, k, bank, slots=slice(0, N)):
            codes, scales = xm_blocks[b][k]
            nc.tensor.matmul_mx(
                out=bank[:, slots], lhsT=codes.bitcast(E4M3), lhsT_scale=scales,
                rhs=h_mx[b][0][:, slots].bitcast(E5M2), rhs_scale=h_mx[b][1][:, slots], start=True, stop=True,
            )

        def empty(b, k, bank, engine_copy, slots=slice(0, N)):
            engine_copy(out=dw[b][k][:, slots], in_=bank[:, slots])

        def scatter_on_vector(b, k):
            nc.vector.tensor_copy(out=windows[k][:].indirect(listed(b, 0, N)), in_=dw[b][k][:])

        def scatter_half(b, k, part, values):
            nc.scalar.activation(out=windows[k][:].indirect(listed(b, part * HALF, HALF)), in_=values, func=ACT.Copy)

        def scatter_both(first, count):
            nc.scalar.activation(
                out=windows[2][:].indirect(listed(0, first, count)), in_=dw_both[:, first : first + count], func=ACT.Copy
            )

        def scatter_on_scalar(b, k):
            for part in range(2):
                scatter_half(b, k, part, dw[b][k][:, half(part)])

        def store(k, queue):
            queue.dma_start(out=out[block(k), :], in_=windows[k][:])

        scalar_copy, vector_copy = nc.scalar.copy, nc.vector.tensor_copy

        zero(windows[0])
        gather_scales()
        gather_ts(0)
        turn_ts(0, banks[4])
        keep_ts(ts_inner0, banks[4])
        keep_ts(ts_outer[0], banks[4])
        gather_ts(1)
        spread_wt(0)
        spread_wt(1)
        interleave(vector_copy, x0_grp[:], x0_raw[:])
        quantize(x_mx[0], slice(0, R), x0_grp[:], E4M3)
        for k in range(2):
            gather_words(0, k * HALF, HALF)
        gather_words(1, 0, N)
        zero(windows[3])
        interleave(vector_copy, x1_grp[0][:], x1_raw[0][:])
        zero(windows[1])

        for c in range(BLOCKS):
            scores(0, c, banks[c])
            sigmoid(0, c, banks[c])
        for c in range(BLOCKS):
            turn_y(0, c, banks[c])
        interleave(scalar_copy, x1_grp[1][:], x1_raw[1][:])
        subtract(0, 0, banks[0])
        turn_ts(1, banks[0])
        keep_ts(ts_outer[1], banks[0])
        subtract(0, 1, banks[1])
        weigh(0, 0)
        turn_h(0, 0, banks[4])
        group_h(0, 0, banks[4], scalar_copy)
        weigh(0, 1)
        turn_h(0, 1, banks[6])
        group_h(0, 1, banks[6], scalar_copy)
        for k in (1, 0):
            quantize(x_mx[1], half(k), x1_grp[k][:], E4M3)
        interleave_on_gpsimd(xm0_grp[0], xm0_raw[0])
        for c, bank in enumerate((banks[0], banks[1], banks[4], banks[6])):
            scores(1, c, bank)
            sigmoid(1, c, bank)
        subtract(0, 2, banks[2])
        subtract(0, 3, banks[3])
        weigh(0, 2)
        turn_h(0, 2, banks[2])
        weigh(0, 3)
        turn_h(0, 3, banks[3])
        quantize_h(0, 0)
        group_h(0, 2, banks[2], vector_copy)
        quantize(xm0_mx[0], slice(0, HALF), xm0_grp[0][:], E4M3)
        product(0, 0, banks[7], half(0))
        empty(0, 0, banks[7], scalar_copy, half(0))
        scatter_half(0, 0, 0, dw[0][0][:, half(0)])
        y_banks = (banks[4], banks[2], banks[3], banks[4])
        turn_y(1, 0, y_banks[0])
        turn_y(1, 1, y_banks[1])
        group_h(0, 3, banks[3], vector_copy)
        quantize_h(0, 1)
        interleave_on_gpsimd(xm0_grp[1], xm0_raw[1])
        interleave_on_gpsimd(xm1_grp, xm1_raw)
        product(0, 0, banks[0], half(1))
        turn_y(1, 2, y_banks[2])

        subtract(1, 0, y_banks[0])
        turn_y(1, 3, y_banks[3])
        product(0, 1, banks[1])
        subtract(1, 1, y_banks[1])
        weigh(1, 0)
        turn_h(1, 0, banks[6])
        weigh(1, 1)
        turn_h(1, 1, banks[2])
        subtract(1, 2, y_banks[2])
        group_h(1, 0, banks[6], vector_copy)
        subtract(1, 3, y_banks[3])
        group_h(1, 1, banks[2], vector_copy)
        weigh(1, 2)
        turn_h(1, 2, banks[3])
        weigh(1, 3)
        turn_h(1, 3, banks[4])
        quantize_h(1, 0)
        quantize(xm0_mx[1], slice(0, HALF), xm0_grp[1][:], E4M3)
        product(0, 3, banks[7])
        quantize(xm1_mx, slice(0, D), xm1_grp[:], E4M3)
        group_h(1, 2, banks[3], vector_copy)
        group_h(1, 3, banks[4], vector_copy)
        quantize_h(1, 1)
        zero(windows[2])

        def on_scalar(b, k, bank):
            product(b, k, bank)
            empty(b, k, bank, scalar_copy)
            scatter_on_scalar(b, k)

        empty(0, 0, banks[0], scalar_copy, half(1))
        scatter_half(0, 0, 1, dw[0][0][:, half(1)])
        empty(0, 1, banks[1], scalar_copy)
        scatter_on_scalar(0, 1)
        on_scalar(1, 0, banks[0])
        store(0, nc.scalar)
        empty(0, 3, banks[7], vector_copy)
        scatter_on_vector(0, 3)
        for k, bank in ((3, banks[6]), (1, banks[2])):
            product(1, k, bank)
            empty(1, k, bank, vector_copy)
            scatter_on_vector(1, k)
            store(k, nc.sync)
        for b, bank in enumerate((banks[1], banks[5])):
            product(b, 2, bank)
            empty(b, 2, bank, scalar_copy)
        for first in range(0, B * N, LONG):
            scatter_both(first, min(LONG, B * N - first))
        store(2, nc.scalar)
